import numpy as np, ml_dtypes
CORES = [5,29,101,125,133,157,229,253]
N = 8
import mx_ref
BF = ml_dtypes.bfloat16
def gcols(t, e):
    v = np.concatenate([t.reshape(8, 16, -1, 4), np.zeros((8, 16, 1, 4), BF)], axis=2)
    return np.ascontiguousarray(np.stack([v[g][:, e[g]] for g in range(8)])).reshape(128, -1)
def tile(rs):
    return np.stack(rs, axis=2).reshape(128, -1).astype(BF)
def pick(q, e):
    c = np.concatenate([q[0].reshape(128, -1, 4), np.zeros((128, 1, 4), np.uint8)], axis=1); s = np.concatenate([q[1], np.ones((16, 1), np.uint8)], axis=1)
    return (np.ascontiguousarray(c[:, e].reshape(128, -1)), np.ascontiguousarray(s[:, e]))
def join(*qs):
    return (np.concatenate([q[0] for q in qs], axis=1), np.concatenate([q[1] for q in qs], axis=1))
def put(q, e, v):
    c, s = q[0].reshape(128, -1, 4).copy(), q[1].copy(); c[:, e] = v[0].reshape(128, -1, 4); s[:, e] = v[1]
    return (c.reshape(128, -1), s)
def pk(c, s):
    return (np.ascontiguousarray(c), mx_ref.live(s))
def emit(q):
    return q[0], q[1]
def packed(v, rng):
    q = [mx_ref.quantize(np.ascontiguousarray(v[r])) for r in range(N)]
    return np.stack([a for a, b in q]), np.stack([mx_ref.plane(b, rng) for a, b in q])
def values_of_codes():
    e, c = np.zeros((128, 128, 4), np.float32), np.zeros((128, 2, 4), np.uint8)
    e[np.arange(128), np.arange(128), 0] = 1
    c[:127, :, 0] = np.arange(256).reshape(2, 128).T[:127]
    return mx_ref.matmul(mx_ref.quantize(e.reshape(128, 512).astype(BF)), (c.reshape(128, 8), np.full((16, 2), 127, np.uint8))).T.reshape(-1).astype(np.float64)
CODE_VALUE, SCALE_VALUE = values_of_codes(), 2.0 ** (np.arange(256) - 127.0)
def decode(q):
    return (CODE_VALUE[q[0]].reshape(16, 8, -1, 4) * SCALE_VALUE[q[1]][:, None, :, None] + 0.0).reshape(128, -1).astype(np.float32)
def f(rng, *shape):
    return mx_ref.flush((rng.standard_normal(shape, dtype=np.float32) * np.exp2(rng.integers(-2, 3, shape[:-1] + (1,)))).astype(BF))
def wide(rng, *shape, cols=0):
    v = rng.standard_normal(shape, dtype=np.float32) * np.exp2(rng.integers(-12, 13, shape)).astype(np.float32)
    if cols: v *= np.repeat(np.exp2(rng.integers(-cols, cols + 1, shape[:-2] + (1, shape[-1] // 4))) * (rng.random(shape[:-2] + (1, shape[-1] // 4)) > 0.0625), 4, axis=-1).astype(np.float32)
    return mx_ref.flush(v.astype(BF))
C, H = 448, 224
def order(p):
    return np.argsort(p[::16] + np.float32(0.0), axis=1, kind="stable")
def places(e):
    at = np.full((8, C + H), -1)
    np.put_along_axis(at, e, np.tile(np.arange(C), (8, 1)), axis=1)
    return at
def mean(a, b):
    return ((a.astype(np.float32) + b.astype(np.float32)) * np.float32(0.5)).astype(BF)
def layer(w, q):
    return tile([mx_ref.matmul(pick(w, np.arange(128 * b, 128 * b + 128)), q) * np.float32(0.03125) for b in range(4)])
def big(v, k=1):
    v = v.astype(np.float32) * np.float32(k)
    v[np.abs(v) < np.float32(2.0 ** -16)] = 0
    return v.astype(BF)
def numbers_of(rng):
    return {"x": big(f(rng, N, 128, 4 * C)), "u": np.array(f(rng, N, 128, 512)), "v": np.array(f(rng, N, 128, 512))}
def weights(rng, w):
    c, p = packed(w, rng)
    return {"wc": c, "ws": p}
def still(rng):
    w = np.zeros((N, 128, 4, 128, 4), np.float32)
    i = np.arange(128)
    for b in range(4): w[:, i, b, i, b] = 32
    return weights(rng, w.reshape(N, 128, 2048).astype(BF))
def signs(rng):
    g = rng.permutation(8)
    return ((g[None, :] + np.arange(N)[:, None]) % 4 < 2) * 2.0 - 1.0
def setup_inputs(rng):
    return {**numbers_of(rng), **weights(rng, f(rng, N, 128, 2048))}
def setup_inputs_ties(rng):
    d = numbers_of(rng)
    e = rng.permutation(N)
    x = d["x"].reshape(N, 8, 16, C, 4)
    for r in range(N):
        k = np.zeros(C, int) if r == e[0] else rng.permutation(C) % 3
        a = x[r][:, :8, :3].copy()
        a[:, :, 2] = 0
        x[r][:, :8] = a[:, :, k]
    u = d["u"].reshape(N, 8, 16, 128, 4)
    u[:, :, 8:, ::16] = 0
    w = np.array(f(rng, N, 128, 2048)).reshape(N, 8, 16, 4, 8, 16, 4)
    w[:, :, 8:, :, :, :8] = 0
    return {"x": x.reshape(N, 128, 4 * C), "u": u.reshape(N, 128, 512), "v": d["v"], **weights(rng, w.reshape(N, 128, 2048))}
def setup_inputs_near(rng):
    d = numbers_of(rng)
    x = d["x"].astype(np.float32).reshape(N, 8, 16, C, 4)
    s = (C - 1 - np.arange(C)) // 3
    g = ((s[:, None] >> np.arange(8)) & 1) * np.exp2(np.arange(8) - 23.0)
    sign = signs(rng)
    x[:, :, 0] = 0
    x[:, :, 0, :, 0] = sign[:, :, None]
    x[:, :, 8] = g[:, :4]
    x[:, :, 9] = g[:, 4:]
    x[:, :, 10:] = rng.integers(4, 8, (N, 8, 6, C, 4)) * rng.choice([-1.0, 1.0], (N, 8, 6, C, 4)) * 2.0 ** -20
    u = d["u"].reshape(N, 128, 128, 4)
    small = rng.permutation(N) < N // 2
    one = np.where(small, 0.0, 1.0).astype(np.float32).astype(BF)
    k = np.where(small[:, None], sign * 2.0 ** -30, 1.0).astype(np.float32).astype(BF)
    u[:, :, ::16] = 0
    for i in range(8):
        u[:, 16 * i, 16 * i, 0] = one
        u[:, 16 * i + 8:16 * i + 10, 16 * i] = k[:, i][:, None, None]
    return {"x": x.reshape(N, 128, 4 * C).astype(BF), "u": u.reshape(N, 128, 512), "v": d["v"], **still(rng)}
def setup_inputs_huge(rng):
    d = numbers_of(rng)
    x = 2.0 ** 30 * (0.6 + 0.4 * rng.random((N, 128, C, 4)))
    c = np.stack([rng.permutation(C) % 2 * 2.0 - 1.0 for r in range(N)])
    c[(np.arange(N) + rng.integers(N)) % N < N // 2] = 1
    x *= c[:, None, :, None]
    u = d["u"].reshape(N, 128, 128, 4)
    a = 2.0 ** 30 * (1 - 0.25 * rng.random((N, 128, 8, 4))) * signs(rng)[:, None, :, None]
    u[:, :, ::16] = a.astype(np.float32).astype(BF)
    return {"x": x.astype(np.float32).reshape(N, 128, 4 * C).astype(BF), "u": u.reshape(N, 128, 512), "v": d["v"], **still(rng)}
def setup_inputs_sizes(rng):
    d = setup_inputs(rng)
    d["x"] = big(d["x"], np.exp2(rng.permutation(N) * (16 // N))[:, None, None])
    return d
def setup_inputs_spread(rng):
    d = numbers_of(rng)
    d["x"] = big(wide(rng, N, 128, 4 * C, cols=6))
    w = np.array(f(rng, N, 128, 2048)).reshape(N, 128, 4, 8, 16, 4)
    g = rng.integers(0, 8, N)
    for r in range(N): w[r, :, :, g[r]] = 0
    return {**d, **weights(rng, w.reshape(N, 128, 2048))}
def check_inputs(d):
    b = []
    for k in ("x", "u", "v"):
        a = np.abs(d[k].astype(np.float32))
        if not (np.isfinite(a).all() and ((a == 0) | (a >= 2.0 ** -30) & (a <= 2.0 ** 30)).all()): b.append("a value of " + k)
    if ((d["wc"] == 0x7F) | (d["wc"] == 0xFF)).any(): b.append("a code of wc")
    least, most = [int(mx_ref.quantize(np.full((128, 16), k, np.float32).astype(BF))[1][0, 0]) for k in (2.0 ** -30, 2.0 ** 30)]
    for p in d["ws"]:
        s = mx_ref.live(p)
        if ((s != 1) & ((s < least) | (s > most))).any(): b.append("a scale of ws")
    return b
def reference(x, u, v, wc, ws):
    qu = [mx_ref.quantize(u[r]) for r in range(N)]
    lay = [pk(wc[r], ws[r]) for r in range(N)]
    own, score, lists = [], [], []
    for r in range(N):
        q = mx_ref.quantize(x[r])
        own.append(decode(q).astype(BF))
        score.append(mx_ref.matmul(qu[r], q))
        lists.append([order(score[r])])
    held = [own[r] for r in range(N)]
    for t in range(2):
        pairs = []
        for r in range(N):
            e = lists[r][t]
            pairs.append(mx_ref.quantize(mean(gcols(held[r], e[:, ::2]), gcols(held[r], e[:, 1::2]))))
        for r in range(N):
            q = mx_ref.quantize(layer(lay[r], pairs[(r - 1) % N]))
            held[r] = np.concatenate([own[r], decode(q).astype(BF)], axis=1)
            lists[r].append(order(np.concatenate([score[r], mx_ref.matmul(qu[r], q)], axis=1))[:, :C])
    half = np.tile(np.arange(C) // 2, (8, 1))
    value, used = [], []
    for r in range(N):
        first = layer(lay[r], mx_ref.quantize(gcols(held[r], lists[r][2][:, :H])))
        value.append(np.concatenate([first, np.zeros((128, 4 * (C - H)), BF)], axis=1))
        used.append(np.tile((np.arange(C) < H).astype(np.int64), (8, 1)))
    now = [own[r] for r in range(N)]
    count = [np.zeros((8, C), np.int64) for r in range(N)]
    for t in (2, 1, 0):
        back, flag = [], []
        for r in range(N):
            at = places(lists[r][t])
            is_used = np.take_along_axis(np.concatenate([used[r], np.zeros((8, 1), np.int64)], axis=1), at, axis=1)
            now[r] = mean(now[r], gcols(value[r], at[:, :C]))
            count[r] = count[r] + is_used[:, :C]
            if t > 0:
                back.append(mx_ref.quantize(gcols(value[r], at[:, C:])))
                flag.append(is_used[:, C:])
        if t > 0:
            for r in range(N):
                e = (r + 1) % N
                value[r] = gcols(decode(back[e]).astype(BF), half)
                used[r] = np.take_along_axis(flag[e], half, axis=1)
    y, uc = np.zeros((N, 128, C), np.float32), np.zeros((N, 8, C), np.float32)
    oc, osc = np.zeros((N, 128, 4 * C), np.uint8), np.zeros((N, 16, C), np.uint8)
    for r in range(N):
        q = mx_ref.quantize(now[r])
        y[r] = mx_ref.matmul(mx_ref.quantize(v[r]), q)
        uc[r] = count[r]
        oc[r], osc[r] = emit(q)
    return {"y": y, "uc": uc, "oc": oc, "osc": osc}

@@ -1,0 +1,634 @@
+from concourse.bass import DstId, RemoteDMATransfer
+from concourse.mybir import dt, AluOpType, ActivationFunctionType
+
+OP = AluOpType
+AF = ActivationFunctionType
+C, H = 448, 224
+HW = 688
+OW = 464
+VW = 240
+BIG = 1.0e29
+SH = 2.0 ** -20
+NV0 = (5, 22)
+NVM = (3, 10)
+F32, BF, U16, I32, FP4, U8, F16 = "float32", "bfloat16", "uint16", "int32", "float8_e4m3fn_x4", "uint8", "float16"
+
+
+def _sb(n, d):
+    return ("sbuf", [128, n], d)
+
+
+SCRATCH = {
+    "ps": ("psum", [128, 4096], F32),
+    "xt": _sb(4 * C, BF), "ut": _sb(512, BF), "vt": _sb(512, BF),
+    "qx": _sb(C, FP4), "sx": _sb(C, U8), "qu": _sb(128, FP4), "su": _sb(128, U8), "qr": _sb(128, FP4), "sr": _sb(128, U8),
+    "qv": _sb(128, FP4), "sv": _sb(128, U8), "qw": _sb(512, FP4), "sw": _sb(512, U8),
+    "et": _sb(2048, BF), "qe": _sb(512, FP4), "se": _sb(512, U8), "ones": _sb(128, BF), "idn": _sb(128, BF),
+    "pc": _sb(1, I32), "ci": _sb(2, I32), "cf": _sb(16, F32), "tm": _sb(464, BF), "jrow": _sb(C, F32),
+    "mask": _sb(464, BF), "nmask": _sb(C, BF), "cdg": _sb(H, BF), "cd1": _sb(H, BF), "cd2": _sb(H, BF),
+    "c32": _sb(C, BF), "c16": _sb(H, BF), "idr": _sb(H, BF),
+    "iot": _sb(128, F32), "uoff": _sb(8, U16), "coff": _sb(112, U16),
+    "row0": _sb(C, F32), "row1": _sb(H, F32), "row2": _sb(H, F32), "mm": _sb(C, F32),
+    "hold0": _sb(C, F32), "hold1": _sb(H, F32), "hold2": _sb(H, F32), "eq": _sb(C, BF), "eup": _sb(C, BF),
+    "fl": _sb(20 * C, BF), "sc": _sb(20 * H, F16), "sg": _sb(14 * C, BF),
+    "sm": _sb(512, F32), "of": _sb(384, U16), "si": _sb(192, I32),
+    "g0": _sb(C, F32), "g1": _sb(672, BF), "g2": _sb(496, BF), "dg": _sb(C, F32), "dgb": _sb(5 * C, BF),
+    "cum": _sb(C, F16), "dgc": _sb(C, F16),
+    "srow": _sb(512, F32), "shold": _sb(C, F32), "srtw": _sb(32, F32), "sig1": _sb(C, F32), "sig2": _sb(H, F32),
+    "pdup": _sb(C, F32), "f1": _sb(C, BF), "f1s": _sb(C, BF), "f2": _sb(C, BF), "f2t": _sb(C, BF), "f2s": _sb(C, BF),
+    "at1": _sb(HW, BF), "at2": _sb(HW, BF), "ag1": _sb(C, BF), "ag2": _sb(C, BF),
+    "tph": _sb(4 * C, BF), "t8": _sb(4 * C, BF), "hp": _sb(4 * HW, BF), "ho": _sb(4 * OW, BF), "ztmp": _sb(4 * H, BF),
+    "z1": _sb(4 * H, BF), "z2": _sb(4 * H, BF), "p1": _sb(4 * H, BF), "p2": _sb(4 * H, BF), "e2": _sb(4 * H, BF),
+    "b2": _sb(4 * H, BF), "b1": _sb(4 * H, BF), "xf": _sb(4 * C, BF), "y2": _sb(4 * C, BF), "y1": _sb(4 * C, BF),
+    "v8": _sb(4 * VW, BF), "d1": _sb(4 * VW, BF), "d0": _sb(4 * VW, BF),
+    "qa": _sb(3 * H, FP4), "sa": _sb(3 * H, U8), "qp1": _sb(H, FP4), "sp1": _sb(H, U8), "qp2": _sb(H, FP4), "sp2": _sb(H, U8),
+    "qb2": _sb(H, FP4), "sb2": _sb(H, U8), "qb1": _sb(H, FP4), "sb1": _sb(H, U8), "qo": _sb(C, FP4), "so": _sb(C, U8),
+    "rq": _sb(C + 3 * H, FP4), "rs": _sb(C + 3 * H, U8), "lq": _sb(C + 3 * H, FP4), "ls": _sb(C + 3 * H, U8),
+    "rl": _sb(112, U16), "ll": _sb(112, U16),
+    "mr": _sb(3 * VW, BF), "ix": _sb(2 * C, BF), "un": _sb(5 * C, BF), "ucr": _sb(C, F32), "yo": _sb(C, F32),
+}
+MSGS = ["mx", "l0", "mp", "l1", "k1", "k2", "m2", "m1"]
+SEMAPHORES = (["cV", "cS", "cT", "cG", "lsent", "a_k3"] + ["r_" + m for m in MSGS] + ["a_" + m for m in MSGS] + ["r_mx2"]
+              + ["d%d" % i for i in range(24)])
+BASE = {"mx": 0, "mp": C, "m2": C + H, "m1": C + 2 * H, "l0": 0, "l1": 32, "k1": 64, "k2": 80, "k3": 96}
+FORWARD = ("mx", "l0", "mp", "l1")
+
+
+def R(name, lo, hi, step=1):
+    return (name, lo, hi, step)
+
+
+def bank(b, n, lo=0):
+    return ("ps", 512 * b + lo, 512 * b + n, 1)
+
+
+def pieces(msg):
+    if msg == "mx":
+        return [[(i, "q", 112 * i, 112 * i + 112, "r_mx") for i in range(4)], [(1, "s", 0, C, "r_mx2")]]
+    if msg in ("mp", "m2", "m1"):
+        return [[(0, "q", 0, 112, "r_" + msg), (2, "q", 112, H, "r_" + msg)], [(1, "s", 0, H, "r_" + msg)]]
+    if msg in ("l0", "l1"):
+        return [[(0, "l", 0, 28, "r_" + msg)]]
+    return [[(3, "l", 0, 14, "r_" + msg)]]
+
+
+def relays_of(rank_core, far, topo):
+    cs = [c for c in topo.cores_of(rank_core) if c != rank_core and topo.may_write(c, far)]
+    near = [c for c in cs if topo.die(c) == topo.die(rank_core)]
+    return near + [c for c in cs if c not in near]
+
+
+def side(T, kind, who, lo, hi):
+    ap = T[who + kind][:, lo:hi]
+    return ap.bitcast(dt.uint8) if kind == "q" else ap
+
+
+def mask_of(engines):
+    m = 0
+    for e in engines:
+        m |= 1 << e
+    return m
+
+
+def relay_program(g, core, T, topo):
+    owner = [c for c in topo.cores_of(core) if T.rank_of(c) is not None]
+    if not owner:
+        return
+    rank = T.rank_of(owner[0])
+    n = len(T.cores)
+    nxt, prv = T.cores[(rank + 1) % n], T.cores[(rank - 1) % n]
+    rel = relays_of(owner[0], nxt, topo)
+    if core not in rel:
+        return
+    me = rel.index(core)
+    sent = 0
+    for msg in MSGS:
+        dst = nxt if msg in FORWARD else prv
+        for call in pieces(msg):
+            for (i, kind, lo, hi, sem) in call:
+                if i != me:
+                    continue
+                g.wait_ge(T.sem[sem], len(topo.engines(owner[0], core)) // len(call))
+                rid, pid = topo.addr(dst, core)
+                b = BASE[msg]
+                g.remote_dma(side(T, kind, "l", b + lo, b + hi), side(T, kind, "r", b + lo, b + hi), T.sem["a_" + msg], T.sem.lsent,
+                             pid, rid, topo.mask(core, dst))
+                sent += len(topo.engines(core, dst))
+    g.wait_ge(T.sem.lsent, sent)
+
+
+def make_builder(g, T):
+    ops, acc, sent = [], {}, [0]
+    Q = {"V": g.vector, "S": g.scalar, "T": g.tensor, "G": g, "Y": g.sync}
+    ndma = [0]
+
+    def cols(r):
+        if r[0] == "ps":
+            return {r[1] // 512}
+        return set(range(r[1], r[2], r[3]))
+
+    def add(q, fn, reads, writes, dma=False, remote=False):
+        i = len(ops)
+        deps = set()
+        for r, w in [(r, False) for r in reads] + [(r, True) for r in writes]:
+            cs = cols(r)
+            lst = acc.setdefault(r[0], [])
+            for (ocs, ow, oi, oq) in lst:
+                if oi != i and (w or ow or (r[0] == "ps" and oq != q)) and not cs.isdisjoint(ocs):
+                    deps.add(oi)
+            lst.append((cs, w, i, q))
+        tok = None
+        if dma:
+            tok = ("d%d" % ndma[0], 16)
+            ndma[0] += 1
+        ops.append({"q": q, "fn": fn, "deps": deps, "tok": tok, "need": dma, "plain": not (dma or remote)})
+        return i
+
+    def arrival(sem, val, writes):
+        i = add(None, None, [], writes, remote=True)
+        ops[i]["tok"] = (sem, val)
+
+    def emit():
+        hist = {q: [] for q in Q}
+        for i, o in enumerate(ops):
+            last = {}
+            for d in o["deps"]:
+                if ops[d]["tok"] is None:
+                    last[ops[d]["q"]] = max(last.get(ops[d]["q"], -1), d)
+            q = o["q"]
+            if q in last and len(hist[q]) >= 3:
+                last[q] = max(last[q], hist[q][-3])
+            o["deps"] = [d for d in o["deps"] if ops[d]["tok"] is not None] + list(last.values())
+            if q is not None and o["plain"]:
+                hist[q].append(i)
+        seen = {q: {} for q in Q}
+        for i, o in enumerate(ops):
+            if o["q"] is None:
+                o["clock"] = {("t", i): 1}
+                continue
+            k = seen[o["q"]]
+            keep = []
+            for d in sorted(o["deps"], reverse=True):
+                key, val = (("t", d), 1) if ops[d]["tok"] is not None else (ops[d]["q"], d)
+                if k.get(key, -1) >= val:
+                    continue
+                keep.append(d)
+                ops[d]["need"] = True
+                for kk, vv in ops[d]["clock"].items():
+                    if k.get(kk, -1) < vv:
+                        k[kk] = vv
+            o["deps"] = keep
+            o["clock"] = dict(k)
+            if o["tok"] is not None:
+                o["clock"][("t", i)] = 1
+            else:
+                o["clock"][o["q"]] = i
+        count = {q: 0 for q in Q}
+        for o in ops:
+            if o["q"] is not None and o["tok"] is None and o["need"]:
+                count[o["q"]] += 1
+                o["tok"] = ("c" + o["q"], count[o["q"]])
+                o["inc"] = 1
+        final = {}
+        for o in ops:
+            if o["tok"] is not None:
+                final[o["tok"][0]] = o["tok"][1]
+            if o["q"] is None:
+                continue
+            for d in o["deps"]:
+                Q[o["q"]].wait_ge(T.sem[ops[d]["tok"][0]], ops[d]["tok"][1])
+            ins = o["fn"](Q[o["q"]])
+            if o["need"]:
+                ins.then_inc(T.sem[o["tok"][0]], o.get("inc", 16))
+        final["lsent"] = sent[0]
+        for s, v in final.items():
+            g.wait_ge(T.sem[s], v)
+
+    return add, arrival, emit, sent
+
+
+def rank_program(g, core, T, topo):
+    rank = T.rank_of(core)
+    if rank is None:
+        relay_program(g, core, T, topo)
+        return
+    n = len(T.cores)
+    nxt, prv2 = T.cores[(rank + 1) % n], T.cores[(rank - 2) % n]
+    rel = relays_of(core, nxt, topo)
+    add, arrival, emit, sent = make_builder(g, T)
+
+    def ap(r):
+        if len(r) == 2:
+            return ap(r[0]).indirect(ap(r[1]))
+        return T[r[0]][:, r[1]:r[2]:r[3]] if r[3] != 1 else T[r[0]][:, r[1]:r[2]]
+
+    def rd(*rs):
+        out = []
+        for r in rs:
+            if isinstance(r, tuple):
+                out += list(r) if len(r) == 2 else [r]
+        return out
+
+    def val(s):
+        return ap(s) if isinstance(s, tuple) else s
+
+    def ts(out, a, s1, op0, s2=None, op1=None):
+        if op1 is None:
+            add("V", lambda q: q.tensor_scalar(ap(out), ap(a), val(s1), None, op0), rd(a, s1), [out])
+        else:
+            add("V", lambda q: q.tensor_scalar(ap(out), ap(a), val(s1), val(s2), op0, op1), rd(a, s1, s2), [out])
+
+    def tt(out, a, b, op):
+        add("V", lambda q: q.tensor_tensor(ap(out), ap(a), ap(b), op), rd(a, b), [out])
+
+    def cp(out, a):
+        if len(out) == 2:
+            add("V", lambda q: q.tensor_copy(ap(out), ap(a)), rd(a, out[1]), [out[0]])
+        else:
+            add("V", lambda q: q.tensor_copy(ap(out), ap(a)), rd(a), [out])
+
+    def scan(out, a, b, init, op0, op1):
+        add("V", lambda q: q.tensor_tensor_scan(ap(out), ap(a), ap(b), val(init), op0, op1), rd(a, b, init), [out])
+
+    def mset(out, v):
+        add("V", lambda q: q.memset(ap(out), v), [], [out])
+
+    def act(out, a, f=AF.Copy, bias=None, scale=None, accum=None):
+        kw = {}
+        if bias is not None:
+            kw["bias"] = val(bias)
+        if scale is not None:
+            kw["scale"] = val(scale)
+        if accum is not None:
+            kw["accum_out"] = ap(accum)
+        add("S", lambda q: q.activation(ap(out), ap(a), f, **kw), rd(a, bias, scale), [out] + rd(accum))
+
+    def fill(out, v):
+        m = len(range(out[1], out[2], out[3]))
+        act(out, R("tm", 0, m), AF.Identity, v, 0.0)
+
+    def mov(e, out, a, k=None):
+        if e == "S":
+            act(out, a, AF.Copy, scale=k)
+        elif k is None:
+            cp(out, a)
+        else:
+            ts(out, a, k, OP.mult)
+
+    def quant(q_, s_, a):
+        add("V", lambda q: q.quantize_mx(ap(q_), ap(s_), ap(a)), [a], [q_, s_])
+
+    def mm(out, lq, ls, rq, rs):
+        add("T", lambda q: q.matmul_mx(ap(out), ap(lq), ap(ls), ap(rq), ap(rs), True, True), [lq, ls, rq, rs], [out])
+
+    def four(w, q_, s_, m, b0=2):
+        for b in range(4):
+            mm(bank(b0 + b, m), R("q" + w, 128 * b, 128 * b + 128), R("s" + w, 128 * b, 128 * b + 128), q_, s_)
+
+    def iota(out, pat, base, cm=0):
+        kw = {} if out[0] == "pc" else {"allow_small_or_imprecise_dtypes": True}
+        add("G", lambda q: q.iota(ap(out), pat, base, cm, **kw), [], [out])
+
+    def dma(e, out, in_, reads, writes):
+        add(e, lambda q: q.dma_start(out, in_), reads, writes, dma=True)
+
+    def send(msg, src):
+        for call in pieces(msg):
+            eng = topo.engines(core, rel[0])
+            per = len(eng) // len(call)
+            trs, reads = [], []
+            for j, (i, kind, lo, hi, sem) in enumerate(call):
+                name, b0 = src[kind]
+                s = T[name][:, b0 + lo:b0 + hi]
+                rid, pid = topo.addr(rel[i], core)
+                trs.append((s.bitcast(dt.uint8) if kind == "q" else s, side(T, kind, "r", BASE[msg] + lo, BASE[msg] + hi),
+                            T.sem[sem], pid, rid, mask_of(eng[j * per:j * per + per])))
+                reads.append(R(name, b0 + lo, b0 + hi))
+            sent[0] += per * len(call)
+            if len(trs) == 1:
+                t = trs[0]
+                add("G", lambda q, t=t: q.remote_dma(t[1], t[0], t[2], T.sem.lsent, t[3], t[4], t[5]), reads, [], remote=True)
+            else:
+                add("G", lambda q, trs=trs: q.remote_dma_fused(
+                    [RemoteDMATransfer(dst_ids=[DstId(rid=t[4], pnc=t[3])], dma_engine_mask=t[5], remote_sem=t[2], src=t[0], dst=t[1])
+                     for t in trs], local_sem=T.sem.lsent), reads, [], remote=True)
+
+    far = len(topo.engines(rel[0], nxt))
+    for msg in MSGS:
+        ps_ = [p for call in pieces(msg) for p in call]
+        arrival("a_" + msg, far * len(ps_), [R("l" + k, BASE[msg] + lo, BASE[msg] + hi) for (i, k, lo, hi, s) in ps_])
+    arrival("a_k3", len(topo.engines(T.cores[(rank + 2) % n], core)), [R("ll", BASE["k3"], BASE["k3"] + 14)])
+
+    def col(j):
+        return R("cf", j, j + 1)
+
+    smp, ofp, sip = [0], [0], [0]
+
+    def sm(w):
+        smp[0] += w
+        return R("sm", smp[0] - w, smp[0])
+
+    def of(w):
+        ofp[0] += w
+        return R("of", ofp[0] - w, ofp[0])
+
+    def sub(r, lo, hi, step=1):
+        return R(r[0], r[1] + lo, r[1] + hi, step)
+
+    def plane(name, w, t, lo=0, hi=None, step=1):
+        return R(name, w * t + lo, w * t + (w if hi is None else hi), step)
+
+    def word(name, t, lo, hi):
+        return R(name, 4 * lo + t, 4 * hi, 4)
+
+    dma("S", T.ut[:], T.u[:], [], [R("ut", 0, 512)])
+    for j in range(2):
+        dma("Y", T.xt[:, 4 * H * j:4 * H * j + 4 * H], T.x[:, 4 * H * j:4 * H * j + 4 * H], [], [R("xt", 4 * H * j, 4 * H * j + 4 * H)])
+    iota(R("pc", 0, 1), [[0, 1]], 0, 1)
+    iota(R("tm", 0, 464), [[0, 29], [1, 16]], 0)
+    iota(R("iot", 0, 8), [[16, 8]], 0)
+    mset(R("ones", 0, 128), 1.0)
+    mset(R("et", 0, 2048), 0.0)
+    add("G", lambda q: q.affine_select(T.idn[:], T.ones[:], [[-1, 128]], OP.is_equal, 0.0, 0, 1), [R("ones", 0, 128)], [R("idn", 0, 128)])
+    iota(R("iot", 78, 106), [[16, 28]], 16)
+    iota(R("iot", 8, 36), [[16, 14], [0, 2]], 15)
+    iota(R("iot", 36, 50), [[16, 14]], 15)
+    iota(R("iot", 50, 78), [[0, 14], [256, 2]], 15)
+    iota(R("jrow", 0, C), [[1, C]], 1)
+    ts(R("ci", 0, 1), R("pc", 0, 1), 15, OP.bitwise_and)
+    ts(R("ci", 1, 2), R("pc", 0, 1), 4, OP.logical_shift_right, 1, OP.bitwise_and)
+    cp(R("cf", 0, 2), R("ci", 0, 2))
+    ts(R("mask", 0, 464), R("tm", 0, 464), col(0), OP.is_equal)
+    ts(R("nmask", 0, C), R("tm", 0, C), col(0), OP.not_equal)
+    cp(R("uoff", 0, 8), R("iot", 0, 8))
+    act(R("cd1", 0, H), R("mask", 15, 15 + H), AF.Identity, 1.0, -(1.0 - SH))
+    act(R("cd2", 0, H), R("mask", 16, 16 + H), AF.Copy, None, 2.0 ** 60)
+    for b in range(4):
+        act(R("et", 512 * b + b, 512 * b + 512, 4), R("idn", 0, 128))
+    tt(R("cdg", 0, H), R("cd1", 0, H), R("cd2", 0, H), OP.max)
+    quant(R("qu", 0, 128), R("su", 0, 128), R("ut", 0, 512))
+    add("V", lambda q: q.tensor_copy(T.qr[:, 0:128].bitcast(dt.uint32), T.qu[:, 0:128].bitcast(dt.uint32).indirect(T.uoff[:, 0:8])),
+        [R("qu", 0, 128), R("uoff", 0, 8)], [R("qr", 0, 128)])
+    add("S", lambda q: q.activation(T.sr[:, 0:128], T.su[:, 0:128].indirect(T.uoff[:, 0:8]), AF.Copy),
+        [R("su", 0, 128), R("uoff", 0, 8)], [R("sr", 0, 128)])
+    act(col(3), R("mask", 15, 16), AF.Identity, 1.0 / SH, 1.0 - 1.0 / SH)
+    for j in range(2):
+        quant(R("qx", H * j, H * j + H), R("sx", H * j, H * j + H), R("xt", 4 * H * j, 4 * H * j + 4 * H))
+    dma("Y", T.qw[:].bitcast(dt.uint8), T.wc[:], [R("xt", 4 * C - 1, 4 * C)], [R("qw", 0, 512)])
+    dma("Y", T.sw[:], T.ws[:], [], [R("sw", 0, 512)])
+    dma("Y", T.vt[:], T.v[:], [], [R("vt", 0, 512)])
+    qr, sr = R("qr", 0, 128), R("sr", 0, 128)
+    mm(bank(0, C), qr, sr, R("qx", 0, C), R("sx", 0, C))
+    mm(bank(1, C), qr, sr, R("qx", 0, C), R("sx", 0, C))
+    send("mx", {"q": ("qx", 0), "s": ("sx", 0)})
+    quant(R("qe", 0, 512), R("se", 0, 512), R("et", 0, 2048))
+
+    def ranks(m, b_v, b_s, row, hold, nv, between, extra):
+        nk, h = m // 16, m // 2
+        vs = list(range(nv[0], nv[1]))
+        ss = [k for k in range(nk) if k not in vs]
+        act(R(row, 0, m), bank(b_s, m))
+        tt(R("mm", 0, m), bank(b_v, m), R("mask", 16, 16 + m), OP.mult)
+        scan(R(hold, 0, m), R("nmask", 0, m), R("mm", 0, m), 0.0, OP.mult, OP.add)
+        lt, gt, init, base, dif, out, off = sm(nk), sm(nk), sm(nk), sm(nk), sm(nk), sm(nk), of(nk)
+        for j, k in enumerate(ss):
+            act(R("sg", m * j, m * j + m), R(row, 0, m), AF.Sign, R(hold, 16 * k + 15, 16 * k + 16), -1.0)
+            between.get(("S", j), lambda: None)()
+        for j, k in enumerate(ss):
+            lo, hi = R("sg", m * j, m * j + 16 * k + 16), R("sg", m * j + 16 * k + 16, m * j + m)
+            act(lo, lo, AF.Relu, None, -1.0, sub(gt, k, k + 1))
+            if k + 1 < nk:
+                act(hi, hi, AF.Relu, None, None, sub(lt, k, k + 1))
+        between.get("V0", lambda: None)()
+        tt(R("eq", 0, m), bank(b_v, m), R(hold, 0, m), OP.is_equal)
+        for j, k in enumerate(vs):
+            s, e = R(hold, 16 * k + 15, 16 * k + 16), 16 * k + 16
+            ts(R("fl", m * j, m * j + e), R(row, 0, e), s, OP.is_le)
+            ts(R("fl", m * j + e, m * j + m), R(row, e, m), s, OP.is_lt)
+            if j == 0:
+                scan(R("eup", 0, m), R("eq", 0, m), R("nmask", 0, m), 0.0, OP.add, OP.mult)
+                mset(sub(lt, nk - 1, nk), 0.0)
+            between.get(("V", j), lambda: None)()
+        extra(init, R("eup", 15, m, 16))
+        tt(base, init, R("iot", 78, 78 + nk), OP.add)
+        parts = ((0, nv[0]), (nv[1], nk))
+        for j, k in enumerate(vs):
+            scan(R("sc", h * j, h * j + h), R("fl", m * j, m * j + h), R("fl", m * j + h, m * j + m), sub(init, k, k + 1), OP.add, OP.add)
+            for lo, hi in parts:
+                if j == len(vs) - 4:
+                    tt(sub(dif, lo, hi), sub(lt, lo, hi), sub(gt, lo, hi), OP.subtract)
+                if j == len(vs) - 3:
+                    tt(sub(out, lo, hi), sub(dif, lo, hi), sub(base, lo, hi), OP.add)
+                if j == len(vs) - 2:
+                    cp(sub(off, lo, hi), sub(out, lo, hi))
+        ends = R("sc", h - 1, h * len(vs), h)
+        cp(sub(off, nv[0], nv[1]), ends)
+        return out, off, lambda: cp(sub(out, nv[0], nv[1]), ends)
+
+    def diag(out, a):
+        scan(out, R("cdg", 0, H), a, 1.0, OP.mult, OP.min)
+
+    def to_offsets(row, j):
+        o = of(28)
+        for i in range(2):
+            diag(R("dgb", C * j + H * i, C * j + H * i + H), sub(row, H * i, H * i + H))
+        ts(o, R("dgb", C * j + 15, C * j + C, 16), col(3), OP.mult, -1.0, OP.add)
+        return o
+
+    def halved(a, w):
+        i0, i1 = R("si", sip[0], sip[0] + w), R("si", sip[0] + w, sip[0] + 2 * w)
+        sip[0] += 2 * w
+        o = of(w)
+        cp(i0, a)
+        ts(i1, i0, 1, OP.arith_shift_right)
+        ts(o, i1, 224.0, OP.min)
+        return o
+
+    r0, o_r0, r0_done = ranks(C, 0, 1, "row0", "hold0", NV0, {}, lambda init, eup: ts(init, eup, -1.0, OP.mult, -1.0, OP.add))
+    four("e", R("lq", 0, C), R("ls", 0, C), C)
+    cp((R("g0", 0, C), o_r0), R("jrow", 0, C))
+    for t in range(4):
+        act(plane("tph", C, t), bank(2 + t, C), AF.Copy, None, 0.5)
+    diag(R("dg", 0, H), R("g0", 0, C, 2))
+    diag(R("dg", H, C), R("g0", 1, C, 2))
+    l0 = of(28)
+    ts(l0, R("dg", 15, C, 16), col(3), OP.mult, -1.0, OP.add)
+    send("l0", {"l": ("of", l0[1])})
+    four("e", R("qx", 0, C), R("sx", 0, C), C)
+    r0_done()
+    mset(R("srow", C, 512), BIG)
+    cp(R("srow", 0, C, 2), (R("row0", 0, C), sub(l0, 0, 14)))
+    cp(R("srow", 1, C, 2), (R("row0", 0, C), sub(l0, 14, 28)))
+    act(col(4), col(0), AF.Copy, None, 16.0)
+    act(col(5), col(1), AF.Copy, None, 28.0)
+    act(col(6), col(1), AF.Identity, 28.0, -28.0)
+    fill(R("hp", 0, 4 * HW, HW), 0.0)
+    act(R("idr", 0, H), R("jrow", 0, H), AF.Copy, None, 2.0 ** -17)
+    mset(R("srtw", 28, 32), BIG)
+    mset(R("c32", 0, C), 1.0)
+    tt(R("mm", 0, C), R("srow", 0, C), R("mask", 16, 16 + C), OP.mult)
+    x1, x2, xd, xs1, xs2 = R("coff", 0, 28), R("coff", 28, 42), R("coff", 42, 70), R("coff", 70, 98), R("coff", 98, 112)
+    cp(R("coff", 0, 42), R("iot", 8, 50))
+    ts(xd, R("iot", 8, 36), col(0), OP.add, -15.0, OP.add)
+    ts(xs1, R("iot", 50, 78), col(4), OP.add)
+    ts(xs2, R("iot", 50, 78, 2), col(4), OP.add)
+    scan(R("shold", 0, C), R("nmask", 0, C), R("mm", 0, C), 0.0, OP.mult, OP.add)
+    fill(R("c32", 0, C, 32), 0.0)
+    act(R("sig1", 0, C), (R("srow", 0, 512), xs1))
+    for t in range(4):
+        act(plane("t8", C, t), bank(2 + t, C), AF.Copy, None, 0.125)
+    mset(R("g1", 0, 672), 1.0)
+    cp(R("srtw", 0, 28), R("shold", 15, C, 16))
+    mset(R("at1", 0, HW), 225.0)
+    o_r = of(28)
+    ts(o_r, r0, 225.0, OP.add)
+
+    def make_p(lst, win, ww, wn, first, zt, qi, pt, qp, sp):
+        for t in range(4):
+            ev = plane("hp", HW, t, 225, 673, 2) if first else plane("ztmp", H, t)
+            act(ev, (plane(win, ww, t, 0, wn), sub(lst, 0, 14)))
+            tt(word(zt, t, 0, H), (plane(win, ww, t, 0, wn), sub(lst, 14, 28)), ev, OP.add)
+        qz, sz = R("qa", H * qi, H * qi + H), R("sa", H * qi, H * qi + H)
+        quant(qz, sz, R(zt, 0, 4 * H))
+        four("w", qz, sz, H)
+        if first:
+            for t in (0, 1):
+                act(plane("hp", HW, t, 226, 674, 2), (plane(win, ww, t), sub(lst, 14, 28)))
+        for t in range(4):
+            mov("SV"[t % 2], word(pt, t, 0, H), bank(2 + t, H), 0.03125)
+        quant(R(qp, 0, H), R(sp, 0, H), R(pt, 0, 4 * H))
+        mm(bank(6, H), qr, sr, R(qp, 0, H), R(sp, 0, H))
+        mm(bank(7, H), qr, sr, R(qp, 0, H), R(sp, 0, H))
+        if first:
+            for t in (2, 3):
+                act(plane("hp", HW, t, 226, 674, 2), (plane(win, ww, t), sub(lst, 14, 28)))
+
+    def merge(row, hold, w, xo, sig, creset, grow, gw, places):
+        m1 = 14 * w
+        ob, cb, c2 = of(28), sm(14), sm(14)
+        ends = R("f1s", w - 1, m1, w)
+        steps = {
+            "V0": lambda: tt(R("f1", 0, m1), (R(hold, 0, H), xo), R(sig, 0, m1), OP.is_ge),
+            ("S", 0): lambda: act(R("pdup", 0, C), (R(row, 0, H), xd)),
+            ("V", 0): lambda: scan(R("f1s", 0, m1), R(creset, 0, m1), R("f1", 0, m1), 0.0, OP.mult, OP.add),
+            ("V", 1): lambda: (ts(sub(ob, 0, 28, 2), ends, col(5), OP.max), ts(sub(ob, 1, 28, 2), ends, col(6), OP.max),
+                               ts(cb, ends, 16.0, OP.mult, -1.0, OP.add)),
+            ("V", 2): lambda: tt(R("f2", 0, C), (R("srtw", 0, 32), ob), R("pdup", 0, C), OP.is_le),
+            ("V", 3): lambda: add("V", lambda q: q.transpose(T.f2t[:], T.f2[:]), [R("f2", 0, C)], [R("f2t", 0, C)]),
+            ("V", 4): lambda: scan(R("f2s", 0, C), R("c32", 0, C), R("f2t", 0, C), 0.0, OP.mult, OP.add),
+            ("V", 5): lambda: tt(c2, cb, R("f2s", 31, C, 32), OP.add),
+        }
+        a, o_a, done = ranks(H, 6, 7, row, hold, NVM, steps, lambda init, eup: tt(init, c2, eup, OP.subtract))
+        cp((R(grow, 0, gw), o_a), R("idr", 0, H))
+        nk, st = places // 16, places // H
+        scan(R("cum", 0, places), R(grow, 0, places), R(grow, 0, places), 224.0, OP.add, OP.max)
+        for j in range(st):
+            diag(R("dgb", H * j, H * j + H), R(grow, j, places, st))
+        for j in range(st):
+            diag(R("dgc", H * j, H * j + H), R("cum", j, places, st))
+        d1, d2, lst = sm(nk), sm(nk), of(nk)
+        ts(d1, R("dgb", 15, places, 16), 2.0 ** 17, OP.mult)
+        tt(d2, d1, R("dgc", 15, places, 16), OP.min)
+        ts(lst, d2, col(3), OP.mult)
+        return a, lst, done
+
+    make_p(R("ll", 0, 28), "tph", C, C, True, "z1", 0, "p1", "qp1", "sp1")
+    send("mp", {"q": ("qp1", 0), "s": ("sp1", 0)})
+    a1, l1, done = merge("row1", "hold1", 32, x1, "sig1", "c32", "g1", 672, C)
+    send("l1", {"l": ("of", l1[1])})
+    four("e", R("lq", C, C + H), R("ls", C, C + H), H)
+    for t in range(4):
+        act(plane("hp", HW, t, 1, 225), bank(2 + t, H), AF.Copy, None, 0.5)
+    done()
+    cp((R("at1", 0, HW), sub(l1, 0, 14)), R("jrow", 0, H))
+    cp((R("at1", 0, HW), sub(l1, 14, 28)), R("jrow", 0, H))
+    o_b1 = halved(a1, 14)
+    send("k1", {"l": ("of", o_b1[1])})
+    act(R("sig2", 0, H), (R("srow", 0, 512), xs2))
+    fill(R("ho", 0, 4 * OW, OW), 0.0)
+    for nm in ("v8", "d1", "d0"):
+        fill(R(nm, H, 4 * VW, VW), 0.0)
+    fill(R("mr", H, 3 * VW, VW), 225.0)
+    ts(R("c16", 0, H), R("tm", 0, H), 0.0, OP.is_gt)
+    mset(R("g2", 0, 496), 1.0)
+    mset(R("at2", 0, HW), 225.0)
+    for t in range(4):
+        for j in range(2):
+            mov("SV"[t % 2], plane("ho", OW, t, 225 + j, 449, 2), (plane("t8", C, t), sub(l0, 14 * j, 14 * j + 7)), 8.0)
+    act(R("ag1", 0, C), (R("at1", 0, HW), o_r))
+
+    make_p(R("ll", 32, 60), "hp", HW, 673, False, "z2", 1, "p2", "qp2", "sp2")
+    four("e", R("qp2", 0, H), R("sp2", 0, H), H)
+    a2, l2, done = merge("row2", "hold2", 16, x2, "sig2", "c16", "g2", 496, H)
+    for t in range(4):
+        act(plane("ho", OW, t, 1, 225), bank(2 + t, H))
+    for t in range(4):
+        mov("SV"[t % 2], word("e2", t, 0, H), (plane("ho", OW, t, 0, 449), l2))
+    qz, sz = R("qa", 2 * H, 3 * H), R("sa", 2 * H, 3 * H)
+    quant(qz, sz, R("e2", 0, 4 * H))
+    four("w", qz, sz, H)
+    done()
+    o_b2 = of(14)
+    ts(o_b2, a2, 224.0, OP.min)
+    send("k2", {"l": ("of", o_b2[1])})
+    rid, pid = topo.addr(prv2, core)
+    add("G", lambda q: q.remote_dma(T.ll[:, BASE["k3"]:BASE["k3"] + 14], ap(o_b2), T.sem.a_k3, T.sem.lsent, pid, rid, topo.mask(core, prv2)),
+        [o_b2], [], remote=True)
+    sent[0] += len(topo.engines(core, prv2))
+
+    def hand_back(k, bt, qb, sb, msg, vals, kv):
+        for t in range(4):
+            mov("SV"[t % 2], word(bt, t, 0, H), bank(2 + t, H), k)
+        quant(R(qb, 0, H), R(sb, 0, H), R(bt, 0, 4 * H))
+        send(msg, {"q": (qb, 0), "s": (sb, 0)})
+        for t in range(4):
+            act(plane(vals, VW, t, 0, H), bank(2 + t, H), AF.Copy, None, kv)
+
+    def landed(m):
+        return R("ll", BASE[m], BASE[m] + 14)
+
+    hand_back(0.03125, "b2", "qb2", "sb2", "m2", "v8", 2.0 ** -8)
+    cp((R("at2", 0, HW), l2), R("jrow", 0, H))
+    o_x1 = to_offsets(R("ag1", 0, C), 1)
+    act(R("ag2", 0, C), (R("at2", 0, HW), o_r))
+    o_x0 = halved(r0, 28)
+    quant(R("qv", 0, 128), R("sv", 0, 128), R("vt", 0, 512))
+    o_x2 = to_offsets(R("ag2", 0, C), 2)
+    jw = R("jrow", 0, 225)
+    act(plane("mr", VW, 0, 0, H), (jw, landed("k2")))
+    act(R("ix", 0, C), (plane("mr", VW, 0, 0, 225), o_x1))
+    for t in range(4):
+        tt(plane("y2", C, t), (plane("v8", VW, t, 0, 225), o_x2), plane("t8", C, t), OP.add)
+
+    four("e", R("lq", C + H, C + 2 * H), R("ls", C + H, C + 2 * H), H)
+    hand_back(None, "b1", "qb1", "sb1", "m1", "d1", 0.25)
+    o_y1 = to_offsets(R("ix", 0, C), 3)
+    act(plane("mr", VW, 1, 0, H), (jw, landed("k3")))
+    act(plane("mr", VW, 2, 0, H), (plane("mr", VW, 1, 0, 225), landed("k1")))
+    act(R("ix", C, 2 * C), (plane("mr", VW, 2, 0, 225), o_x0))
+    act(R("un", 0, C), R("ag2", 0, C), AF.Relu, -224.0, 1.0)
+    for t in range(4):
+        tt(plane("y1", C, t), (plane("d1", VW, t, 0, 225), o_y1), plane("y2", C, t), OP.add)
+    o_y0 = to_offsets(R("ix", C, 2 * C), 4)
+    for j in range(2):
+        ts(R("un", C + C * j, 2 * C + C * j), R("ix", C * j, C * j + C), 224.0, OP.max, -232.0, OP.add)
+    scan(R("un", 3 * C, 4 * C), R("un", 0, C), R("un", C, 2 * C), -64.0, OP.max, OP.add)
+    scan(R("un", 4 * C, 5 * C), R("un", 3 * C, 4 * C), R("un", 2 * C, 3 * C), -64.0, OP.max, OP.add)
+    act(R("ucr", 0, C), R("un", 4 * C, 5 * C), AF.Identity, -13.0, -1.0)
+    dma("Y", T.uc[:], T.ucr[0:128:16, :], [R("ucr", 0, C)], [])
+
+    four("e", R("lq", C + 2 * H, C + 3 * H), R("ls", C + 2 * H, C + 3 * H), H)
+    for t in range(4):
+        act(plane("d0", VW, t, 0, H), bank(2 + t, H), AF.Copy, None, 0.5)
+    for j in range(2):
+        lo, hi = H * j, H * j + H
+        for t in range(4):
+            tt(word("xf", t, lo, hi), (plane("d0", VW, t, 0, 225), sub(o_y0, 14 * j, 14 * j + 14)), plane("y1", C, t, lo, hi), OP.add)
+        quant(R("qo", lo, hi), R("so", lo, hi), R("xf", 4 * lo, 4 * hi))
+        mm(bank(j, H), R("qv", 0, 128), R("sv", 0, 128), R("qo", lo, hi), R("so", lo, hi))
+        dma("Y", T.oc[:, 4 * lo:4 * hi], T.qo[:, lo:hi].bitcast(dt.uint8), [R("qo", lo, hi)], [])
+        act(R("yo", lo, hi), bank(j, H))
+        dma("S", T.y[:, lo:hi], T.yo[:, lo:hi], [R("yo", lo, hi)], [])
+    for k in range(4):
+        dma("Y", T.osc[4 * k:4 * k + 4, :], T.so[32 * k:32 * k + 4, :], [R("so", 0, C)], [])
+    emit()

@@ -9,8 +9,8 @@ OW = 464
 VW = 240
 BIG = 1.0e29
 SH = 2.0 ** -20
-NV0 = (5, 22)
-NVM = (3, 10)
+NV0 = 16
+NVM = 6
 F32, BF, U16, I32, FP4, U8, F16 = "float32", "bfloat16", "uint16", "int32", "float8_e4m3fn_x4", "uint8", "float16"
 
 
@@ -25,7 +25,7 @@ SCRATCH = {
     "qv": _sb(128, FP4), "sv": _sb(128, U8), "qw": _sb(512, FP4), "sw": _sb(512, U8),
     "et": _sb(2048, BF), "qe": _sb(512, FP4), "se": _sb(512, U8), "ones": _sb(128, BF), "idn": _sb(128, BF),
     "pc": _sb(1, I32), "ci": _sb(2, I32), "cf": _sb(16, F32), "tm": _sb(464, BF), "jrow": _sb(C, F32),
-    "mask": _sb(464, BF), "nmask": _sb(C, BF), "cdg": _sb(H, BF), "cd1": _sb(H, BF), "cd2": _sb(H, BF),
+    "mask": _sb(464, BF), "nmask": _sb(C, BF), "cdg": _sb(H, BF), "cd1": _sb(32, BF), "cd2": _sb(32, BF),
     "c32": _sb(C, BF), "c16": _sb(H, BF), "idr": _sb(H, BF),
     "iot": _sb(128, F32), "uoff": _sb(8, U16), "coff": _sb(112, U16),
     "row0": _sb(C, F32), "row1": _sb(H, F32), "row2": _sb(H, F32), "mm": _sb(C, F32),
@@ -345,11 +345,11 @@ def rank_program(g, core, T, topo):
     for j in range(2):
         dma("Y", T.xt[:, 4 * H * j:4 * H * j + 4 * H], T.x[:, 4 * H * j:4 * H * j + 4 * H], [], [R("xt", 4 * H * j, 4 * H * j + 4 * H)])
     iota(R("pc", 0, 1), [[0, 1]], 0, 1)
-    iota(R("tm", 0, 464), [[0, 29], [1, 16]], 0)
-    iota(R("iot", 0, 8), [[16, 8]], 0)
     mset(R("ones", 0, 128), 1.0)
     mset(R("et", 0, 2048), 0.0)
     add("G", lambda q: q.affine_select(T.idn[:], T.ones[:], [[-1, 128]], OP.is_equal, 0.0, 0, 1), [R("ones", 0, 128)], [R("idn", 0, 128)])
+    iota(R("tm", 0, 464), [[0, 29], [1, 16]], 0)
+    iota(R("iot", 0, 8), [[16, 8]], 0)
     iota(R("iot", 78, 106), [[16, 28]], 16)
     iota(R("iot", 8, 36), [[16, 14], [0, 2]], 15)
     iota(R("iot", 36, 50), [[16, 14]], 15)
@@ -358,72 +358,83 @@ def rank_program(g, core, T, topo):
     ts(R("ci", 0, 1), R("pc", 0, 1), 15, OP.bitwise_and)
     ts(R("ci", 1, 2), R("pc", 0, 1), 4, OP.logical_shift_right, 1, OP.bitwise_and)
     cp(R("cf", 0, 2), R("ci", 0, 2))
+    for b in range(4):
+        act(R("et", 512 * b + b, 512 * b + 512, 4), R("idn", 0, 128))
+    quant(R("qe", 0, 512), R("se", 0, 512), R("et", 0, 2048))
     ts(R("mask", 0, 464), R("tm", 0, 464), col(0), OP.is_equal)
     ts(R("nmask", 0, C), R("tm", 0, C), col(0), OP.not_equal)
     cp(R("uoff", 0, 8), R("iot", 0, 8))
-    act(R("cd1", 0, H), R("mask", 15, 15 + H), AF.Identity, 1.0, -(1.0 - SH))
-    act(R("cd2", 0, H), R("mask", 16, 16 + H), AF.Copy, None, 2.0 ** 60)
-    for b in range(4):
-        act(R("et", 512 * b + b, 512 * b + 512, 4), R("idn", 0, 128))
-    tt(R("cdg", 0, H), R("cd1", 0, H), R("cd2", 0, H), OP.max)
+    act(R("cd1", 0, 32), R("mask", 15, 47), AF.Identity, 1.0, -(1.0 - SH))
+    act(R("cd2", 0, 32), R("mask", 16, 48), AF.Copy, None, 2.0 ** 60)
     quant(R("qu", 0, 128), R("su", 0, 128), R("ut", 0, 512))
     add("V", lambda q: q.tensor_copy(T.qr[:, 0:128].bitcast(dt.uint32), T.qu[:, 0:128].bitcast(dt.uint32).indirect(T.uoff[:, 0:8])),
         [R("qu", 0, 128), R("uoff", 0, 8)], [R("qr", 0, 128)])
     add("S", lambda q: q.activation(T.sr[:, 0:128], T.su[:, 0:128].indirect(T.uoff[:, 0:8]), AF.Copy),
         [R("su", 0, 128), R("uoff", 0, 8)], [R("sr", 0, 128)])
+    tt(R("cdg", 0, 32), R("cd1", 0, 32), R("cd2", 0, 32), OP.max)
+    for lo, hi in ((32, 64), (64, 128), (128, H)):
+        act(R("cdg", lo, hi), R("cdg", 0, hi - lo))
     act(col(3), R("mask", 15, 16), AF.Identity, 1.0 / SH, 1.0 - 1.0 / SH)
-    for j in range(2):
-        quant(R("qx", H * j, H * j + H), R("sx", H * j, H * j + H), R("xt", 4 * H * j, 4 * H * j + 4 * H))
     dma("Y", T.qw[:].bitcast(dt.uint8), T.wc[:], [R("xt", 4 * C - 1, 4 * C)], [R("qw", 0, 512)])
     dma("Y", T.sw[:], T.ws[:], [], [R("sw", 0, 512)])
     dma("Y", T.vt[:], T.v[:], [], [R("vt", 0, 512)])
     qr, sr = R("qr", 0, 128), R("sr", 0, 128)
-    mm(bank(0, C), qr, sr, R("qx", 0, C), R("sx", 0, C))
-    mm(bank(1, C), qr, sr, R("qx", 0, C), R("sx", 0, C))
+    for j in range(2):
+        quant(R("qx", H * j, H * j + H), R("sx", H * j, H * j + H), R("xt", 4 * H * j, 4 * H * j + 4 * H))
+        for b in (6 * j, 6 * j + 1):
+            mm(bank(b, H), qr, sr, R("qx", H * j, H * j + H), R("sx", H * j, H * j + H))
     send("mx", {"q": ("qx", 0), "s": ("sx", 0)})
-    quant(R("qe", 0, 512), R("se", 0, 512), R("et", 0, 2048))
 
-    def ranks(m, b_v, b_s, row, hold, nv, between, extra):
+    def ranks(m, parts, row, hold, nv, between, win, ids):
         nk, h = m // 16, m // 2
-        vs = list(range(nv[0], nv[1]))
-        ss = [k for k in range(nk) if k not in vs]
-        act(R(row, 0, m), bank(b_s, m))
-        tt(R("mm", 0, m), bank(b_v, m), R("mask", 16, 16 + m), OP.mult)
-        scan(R(hold, 0, m), R("nmask", 0, m), R("mm", 0, m), 0.0, OP.mult, OP.add)
+        ns = nk - nv
+        vs, ss = list(range(ns, nk)), list(range(ns))
+        for i, (b_v, b_s) in enumerate(parts):
+            act(R(row, H * i, H * i + H), bank(b_s, H))
+            tt(R("mm", H * i, H * i + H), bank(b_v, H), R("mask", 16, 16 + H), OP.mult)
+            if i == 1:
+                tt(R("eq", 0, H), bank(parts[0][0], H), R(hold, 0, H), OP.is_equal)
+            scan(R(hold, H * i, H * i + H), R("nmask", 0, H), R("mm", H * i, H * i + H), 0.0, OP.mult, OP.add)
         lt, gt, init, base, dif, out, off = sm(nk), sm(nk), sm(nk), sm(nk), sm(nk), sm(nk), of(nk)
+        between.get("S0", lambda: None)()
         for j, k in enumerate(ss):
             act(R("sg", m * j, m * j + m), R(row, 0, m), AF.Sign, R(hold, 16 * k + 15, 16 * k + 16), -1.0)
-            between.get(("S", j), lambda: None)()
         for j, k in enumerate(ss):
             lo, hi = R("sg", m * j, m * j + 16 * k + 16), R("sg", m * j + 16 * k + 16, m * j + m)
             act(lo, lo, AF.Relu, None, -1.0, sub(gt, k, k + 1))
-            if k + 1 < nk:
-                act(hi, hi, AF.Relu, None, None, sub(lt, k, k + 1))
-        between.get("V0", lambda: None)()
-        tt(R("eq", 0, m), bank(b_v, m), R(hold, 0, m), OP.is_equal)
+            act(hi, hi, AF.Relu, None, None, sub(lt, k, k + 1))
+        between.get("V0", lambda i: None)(init)
+        tt(R("eq", m - H, m), bank(parts[-1][0], H), R(hold, m - H, m), OP.is_equal)
         for j, k in enumerate(vs):
             s, e = R(hold, 16 * k + 15, 16 * k + 16), 16 * k + 16
             ts(R("fl", m * j, m * j + e), R(row, 0, e), s, OP.is_le)
-            ts(R("fl", m * j + e, m * j + m), R(row, e, m), s, OP.is_lt)
+            if e < m:
+                ts(R("fl", m * j + e, m * j + m), R(row, e, m), s, OP.is_lt)
             if j == 0:
                 scan(R("eup", 0, m), R("eq", 0, m), R("nmask", 0, m), 0.0, OP.add, OP.mult)
-                mset(sub(lt, nk - 1, nk), 0.0)
-            between.get(("V", j), lambda: None)()
-        extra(init, R("eup", 15, m, 16))
-        tt(base, init, R("iot", 78, 78 + nk), OP.add)
-        parts = ((0, nv[0]), (nv[1], nk))
+            between.get(("V", j), lambda i: None)(init)
+        once = len(parts) == 1
         for j, k in enumerate(vs):
             scan(R("sc", h * j, h * j + h), R("fl", m * j, m * j + h), R("fl", m * j + h, m * j + m), sub(init, k, k + 1), OP.add, OP.add)
-            for lo, hi in parts:
-                if j == len(vs) - 4:
-                    tt(sub(dif, lo, hi), sub(lt, lo, hi), sub(gt, lo, hi), OP.subtract)
-                if j == len(vs) - 3:
-                    tt(sub(out, lo, hi), sub(dif, lo, hi), sub(base, lo, hi), OP.add)
-                if j == len(vs) - 2:
-                    cp(sub(off, lo, hi), sub(out, lo, hi))
-        ends = R("sc", h - 1, h * len(vs), h)
-        cp(sub(off, nv[0], nv[1]), ends)
-        return out, off, lambda: cp(sub(out, nv[0], nv[1]), ends)
+            if j == 0:
+                tt(sub(base, 0, ns), sub(init, 0, ns), R("iot", 78, 78 + ns), OP.add)
+            if once and j == nv - 2:
+                tt(sub(dif, 0, ns), sub(base, 0, ns), sub(gt, 0, ns), OP.subtract)
+        ends = R("sc", h - 1, h * nv, h)
+        if once:
+            tt(sub(out, 0, ns), sub(dif, 0, ns), sub(lt, 0, ns), OP.add)
+            cp(sub(off, ns, nk), ends)
+            cp(sub(off, 0, ns), sub(out, 0, ns))
+            cp((win, off), R(ids, 0, m))
+            return out, lambda: cp(sub(out, ns, nk), ends)
+        cp(sub(off, ns, nk), ends)
+        cp((win, sub(off, ns, nk)), R(ids, 16 * ns, m))
+        tt(sub(dif, 0, ns), sub(base, 0, ns), sub(gt, 0, ns), OP.subtract)
+        cp(sub(out, ns, nk), ends)
+        tt(sub(out, 0, ns), sub(dif, 0, ns), sub(lt, 0, ns), OP.add)
+        cp(sub(off, 0, ns), sub(out, 0, ns))
+        cp((win, sub(off, 0, ns)), R(ids, 0, 16 * ns))
+        return out, None
 
     def diag(out, a):
         scan(out, R("cdg", 0, H), a, 1.0, OP.mult, OP.min)
@@ -444,9 +455,9 @@ def rank_program(g, core, T, topo):
         ts(o, i1, 224.0, OP.min)
         return o
 
-    r0, o_r0, r0_done = ranks(C, 0, 1, "row0", "hold0", NV0, {}, lambda init, eup: ts(init, eup, -1.0, OP.mult, -1.0, OP.add))
+    r0, _ = ranks(C, [(0, 1), (6, 7)], "row0", "hold0", NV0,
+                  {("V", 2): lambda init: ts(init, R("eup", 15, C, 16), -1.0, OP.mult, -1.0, OP.add)}, R("g0", 0, C), "jrow")
     four("e", R("lq", 0, C), R("ls", 0, C), C)
-    cp((R("g0", 0, C), o_r0), R("jrow", 0, C))
     for t in range(4):
         act(plane("tph", C, t), bank(2 + t, C), AF.Copy, None, 0.5)
     diag(R("dg", 0, H), R("g0", 0, C, 2))
@@ -455,7 +466,6 @@ def rank_program(g, core, T, topo):
     ts(l0, R("dg", 15, C, 16), col(3), OP.mult, -1.0, OP.add)
     send("l0", {"l": ("of", l0[1])})
     four("e", R("qx", 0, C), R("sx", 0, C), C)
-    r0_done()
     mset(R("srow", C, 512), BIG)
     cp(R("srow", 0, C, 2), (R("row0", 0, C), sub(l0, 0, 14)))
     cp(R("srow", 1, C, 2), (R("row0", 0, C), sub(l0, 14, 28)))
@@ -482,15 +492,23 @@ def rank_program(g, core, T, topo):
     mset(R("at1", 0, HW), 225.0)
     o_r = of(28)
     ts(o_r, r0, 225.0, OP.add)
+    o_x0 = halved(r0, 28)
+    quant(R("qv", 0, 128), R("sv", 0, 128), R("vt", 0, 512))
 
-    def make_p(lst, win, ww, wn, first, zt, qi, pt, qp, sp):
+    def make_p(lst, win, ww, wn, first, zt, qi, pt, qp, sp, gap1, gap2):
         for t in range(4):
             ev = plane("hp", HW, t, 225, 673, 2) if first else plane("ztmp", H, t)
-            act(ev, (plane(win, ww, t, 0, wn), sub(lst, 0, 14)))
+            if t == 0:
+                st = ev[3]
+                act(R(ev[0], ev[1], ev[1] + 128 * st, st), (plane(win, ww, t, 0, wn), sub(lst, 0, 8)))
+                cp(R(ev[0], ev[1] + 128 * st, ev[2], st), (plane(win, ww, t, 0, wn), sub(lst, 8, 14)))
+            else:
+                act(ev, (plane(win, ww, t, 0, wn), sub(lst, 0, 14)))
             tt(word(zt, t, 0, H), (plane(win, ww, t, 0, wn), sub(lst, 14, 28)), ev, OP.add)
         qz, sz = R("qa", H * qi, H * qi + H), R("sa", H * qi, H * qi + H)
         quant(qz, sz, R(zt, 0, 4 * H))
         four("w", qz, sz, H)
+        gap1()
         if first:
             for t in (0, 1):
                 act(plane("hp", HW, t, 226, 674, 2), (plane(win, ww, t), sub(lst, 14, 28)))
@@ -499,6 +517,7 @@ def rank_program(g, core, T, topo):
         quant(R(qp, 0, H), R(sp, 0, H), R(pt, 0, 4 * H))
         mm(bank(6, H), qr, sr, R(qp, 0, H), R(sp, 0, H))
         mm(bank(7, H), qr, sr, R(qp, 0, H), R(sp, 0, H))
+        gap2()
         if first:
             for t in (2, 3):
                 act(plane("hp", HW, t, 226, 674, 2), (plane(win, ww, t), sub(lst, 14, 28)))
@@ -508,18 +527,18 @@ def rank_program(g, core, T, topo):
         ob, cb, c2 = of(28), sm(14), sm(14)
         ends = R("f1s", w - 1, m1, w)
         steps = {
-            "V0": lambda: tt(R("f1", 0, m1), (R(hold, 0, H), xo), R(sig, 0, m1), OP.is_ge),
-            ("S", 0): lambda: act(R("pdup", 0, C), (R(row, 0, H), xd)),
-            ("V", 0): lambda: scan(R("f1s", 0, m1), R(creset, 0, m1), R("f1", 0, m1), 0.0, OP.mult, OP.add),
-            ("V", 1): lambda: (ts(sub(ob, 0, 28, 2), ends, col(5), OP.max), ts(sub(ob, 1, 28, 2), ends, col(6), OP.max),
-                               ts(cb, ends, 16.0, OP.mult, -1.0, OP.add)),
-            ("V", 2): lambda: tt(R("f2", 0, C), (R("srtw", 0, 32), ob), R("pdup", 0, C), OP.is_le),
-            ("V", 3): lambda: add("V", lambda q: q.transpose(T.f2t[:], T.f2[:]), [R("f2", 0, C)], [R("f2t", 0, C)]),
-            ("V", 4): lambda: scan(R("f2s", 0, C), R("c32", 0, C), R("f2t", 0, C), 0.0, OP.mult, OP.add),
-            ("V", 5): lambda: tt(c2, cb, R("f2s", 31, C, 32), OP.add),
+            "V0": lambda i: tt(R("f1", 0, m1), (R(hold, 0, H), xo), R(sig, 0, m1), OP.is_ge),
+            "S0": lambda: act(R("pdup", 0, C), (R(row, 0, H), xd)),
+            ("V", 0): lambda i: scan(R("f1s", 0, m1), R(creset, 0, m1), R("f1", 0, m1), 0.0, OP.mult, OP.add),
+            ("V", 1): lambda i: (ts(sub(ob, 0, 28, 2), ends, col(5), OP.max), ts(sub(ob, 1, 28, 2), ends, col(6), OP.max),
+                                 ts(cb, ends, 16.0, OP.mult, -1.0, OP.add)),
+            ("V", 2): lambda i: (tt(R("f2", 0, C), (R("srtw", 0, 32), ob), R("pdup", 0, C), OP.is_le),
+                                 tt(c2, cb, R("eup", 15, H, 16), OP.subtract)),
+            ("V", 3): lambda i: add("V", lambda q: q.transpose(T.f2t[:], T.f2[:]), [R("f2", 0, C)], [R("f2t", 0, C)]),
+            ("V", 4): lambda i: scan(R("f2s", 0, C), R("c32", 0, C), R("f2t", 0, C), 0.0, OP.mult, OP.add),
+            ("V", 5): lambda i: tt(i, c2, R("f2s", 31, C, 32), OP.add),
         }
-        a, o_a, done = ranks(H, 6, 7, row, hold, NVM, steps, lambda init, eup: tt(init, c2, eup, OP.subtract))
-        cp((R(grow, 0, gw), o_a), R("idr", 0, H))
+        a, done = ranks(H, [(6, 7)], row, hold, NVM, steps, R(grow, 0, gw), "idr")
         nk, st = places // 16, places // H
         scan(R("cum", 0, places), R(grow, 0, places), R(grow, 0, places), 224.0, OP.add, OP.max)
         for j in range(st):
@@ -532,7 +551,8 @@ def rank_program(g, core, T, topo):
         ts(lst, d2, col(3), OP.mult)
         return a, lst, done
 
-    make_p(R("ll", 0, 28), "tph", C, C, True, "z1", 0, "p1", "qp1", "sp1")
+    make_p(R("ll", 0, 28), "tph", C, C, True, "z1", 0, "p1", "qp1", "sp1",
+           lambda: mset(R("at2", 0, HW), 225.0), lambda: mset(R("g2", 0, 496), 1.0))
     send("mp", {"q": ("qp1", 0), "s": ("sp1", 0)})
     a1, l1, done = merge("row1", "hold1", 32, x1, "sig1", "c32", "g1", 672, C)
     send("l1", {"l": ("of", l1[1])})
@@ -549,15 +569,16 @@ def rank_program(g, core, T, topo):
     for nm in ("v8", "d1", "d0"):
         fill(R(nm, H, 4 * VW, VW), 0.0)
     fill(R("mr", H, 3 * VW, VW), 225.0)
-    ts(R("c16", 0, H), R("tm", 0, H), 0.0, OP.is_gt)
-    mset(R("g2", 0, 496), 1.0)
-    mset(R("at2", 0, HW), 225.0)
+    act(R("c16", 0, H), R("tm", 0, H), AF.Sign)
     for t in range(4):
         for j in range(2):
             mov("SV"[t % 2], plane("ho", OW, t, 225 + j, 449, 2), (plane("t8", C, t), sub(l0, 14 * j, 14 * j + 7)), 8.0)
     act(R("ag1", 0, C), (R("at1", 0, HW), o_r))
 
-    make_p(R("ll", 32, 60), "hp", HW, 673, False, "z2", 1, "p2", "qp2", "sp2")
+    x1o = []
+    make_p(R("ll", 32, 60), "hp", HW, 673, False, "z2", 1, "p2", "qp2", "sp2",
+           lambda: x1o.append(to_offsets(R("ag1", 0, C), 1)), lambda: None)
+    o_x1 = x1o[0]
     four("e", R("qp2", 0, H), R("sp2", 0, H), H)
     a2, l2, done = merge("row2", "hold2", 16, x2, "sig2", "c16", "g2", 496, H)
     for t in range(4):
@@ -571,10 +592,6 @@ def rank_program(g, core, T, topo):
     o_b2 = of(14)
     ts(o_b2, a2, 224.0, OP.min)
     send("k2", {"l": ("of", o_b2[1])})
-    rid, pid = topo.addr(prv2, core)
-    add("G", lambda q: q.remote_dma(T.ll[:, BASE["k3"]:BASE["k3"] + 14], ap(o_b2), T.sem.a_k3, T.sem.lsent, pid, rid, topo.mask(core, prv2)),
-        [o_b2], [], remote=True)
-    sent[0] += len(topo.engines(core, prv2))
 
     def hand_back(k, bt, qb, sb, msg, vals, kv):
         for t in range(4):
@@ -588,15 +605,17 @@ def rank_program(g, core, T, topo):
         return R("ll", BASE[m], BASE[m] + 14)
 
     hand_back(0.03125, "b2", "qb2", "sb2", "m2", "v8", 2.0 ** -8)
+    rid, pid = topo.addr(prv2, core)
+    add("G", lambda q: q.remote_dma(T.ll[:, BASE["k3"]:BASE["k3"] + 14], ap(o_b2), T.sem.a_k3, T.sem.lsent, pid, rid, topo.mask(core, prv2)),
+        [o_b2], [], remote=True)
+    sent[0] += len(topo.engines(core, prv2))
     cp((R("at2", 0, HW), l2), R("jrow", 0, H))
-    o_x1 = to_offsets(R("ag1", 0, C), 1)
     act(R("ag2", 0, C), (R("at2", 0, HW), o_r))
-    o_x0 = halved(r0, 28)
-    quant(R("qv", 0, 128), R("sv", 0, 128), R("vt", 0, 512))
     o_x2 = to_offsets(R("ag2", 0, C), 2)
     jw = R("jrow", 0, 225)
     act(plane("mr", VW, 0, 0, H), (jw, landed("k2")))
     act(R("ix", 0, C), (plane("mr", VW, 0, 0, 225), o_x1))
+    act(R("un", 0, C), R("ag2", 0, C), AF.Relu, -224.0, 1.0)
     for t in range(4):
         tt(plane("y2", C, t), (plane("v8", VW, t, 0, 225), o_x2), plane("t8", C, t), OP.add)
 
@@ -606,28 +625,26 @@ def rank_program(g, core, T, topo):
     act(plane("mr", VW, 1, 0, H), (jw, landed("k3")))
     act(plane("mr", VW, 2, 0, H), (plane("mr", VW, 1, 0, 225), landed("k1")))
     act(R("ix", C, 2 * C), (plane("mr", VW, 2, 0, 225), o_x0))
-    act(R("un", 0, C), R("ag2", 0, C), AF.Relu, -224.0, 1.0)
+    ts(R("un", C, 2 * C), R("ix", 0, C), 224.0, OP.max, -232.0, OP.add)
+    scan(R("un", 3 * C, 4 * C), R("un", 0, C), R("un", C, 2 * C), -64.0, OP.max, OP.add)
     for t in range(4):
         tt(plane("y1", C, t), (plane("d1", VW, t, 0, 225), o_y1), plane("y2", C, t), OP.add)
     o_y0 = to_offsets(R("ix", C, 2 * C), 4)
-    for j in range(2):
-        ts(R("un", C + C * j, 2 * C + C * j), R("ix", C * j, C * j + C), 224.0, OP.max, -232.0, OP.add)
-    scan(R("un", 3 * C, 4 * C), R("un", 0, C), R("un", C, 2 * C), -64.0, OP.max, OP.add)
+    ts(R("un", 2 * C, 3 * C), R("ix", C, 2 * C), 224.0, OP.max, -232.0, OP.add)
     scan(R("un", 4 * C, 5 * C), R("un", 3 * C, 4 * C), R("un", 2 * C, 3 * C), -64.0, OP.max, OP.add)
-    act(R("ucr", 0, C), R("un", 4 * C, 5 * C), AF.Identity, -13.0, -1.0)
-    dma("Y", T.uc[:], T.ucr[0:128:16, :], [R("ucr", 0, C)], [])
 
     four("e", R("lq", C + 2 * H, C + 3 * H), R("ls", C + 2 * H, C + 3 * H), H)
     for t in range(4):
         act(plane("d0", VW, t, 0, H), bank(2 + t, H), AF.Copy, None, 0.5)
-    for j in range(2):
-        lo, hi = H * j, H * j + H
+    act(R("ucr", 0, C), R("un", 4 * C, 5 * C), AF.Identity, -13.0, -1.0)
+    dma("Y", T.uc[:], T.ucr[0:128:16, :], [R("ucr", 0, C)], [])
+    for j, (lo, hi) in enumerate(((0, 320), (320, C))):
         for t in range(4):
-            tt(word("xf", t, lo, hi), (plane("d0", VW, t, 0, 225), sub(o_y0, 14 * j, 14 * j + 14)), plane("y1", C, t, lo, hi), OP.add)
+            tt(word("xf", t, lo, hi), (plane("d0", VW, t, 0, 225), sub(o_y0, lo // 16, hi // 16)), plane("y1", C, t, lo, hi), OP.add)
         quant(R("qo", lo, hi), R("so", lo, hi), R("xf", 4 * lo, 4 * hi))
-        mm(bank(j, H), R("qv", 0, 128), R("sv", 0, 128), R("qo", lo, hi), R("so", lo, hi))
+        mm(bank(j, hi - lo), R("qv", 0, 128), R("sv", 0, 128), R("qo", lo, hi), R("so", lo, hi))
         dma("Y", T.oc[:, 4 * lo:4 * hi], T.qo[:, lo:hi].bitcast(dt.uint8), [R("qo", lo, hi)], [])
-        act(R("yo", lo, hi), bank(j, H))
+        act(R("yo", lo, hi), bank(j, hi - lo))
         dma("S", T.y[:, lo:hi], T.yo[:, lo:hi], [R("yo", lo, hi)], [])
     for k in range(4):
         dma("Y", T.osc[4 * k:4 * k + 4, :], T.so[32 * k:32 * k + 4, :], [R("so", 0, C)], [])

@@ -9,8 +9,18 @@ OW = 464
 VW = 240
 BIG = 1.0e29
 SH = 2.0 ** -20
-NV0 = 16
-NVM = 6
+DROP = -(2.0 ** 30)
+NVA = 8
+EARLY_V, EARLY_S, MID_V, MID_S = 2, 4, 2, 3
+CHUNKS = ((0, 256), (256, 448))
+RUNS = ((0, 128, 0), (128, H, 96))
+SCORES, COPIES = ((6, 7), (0, 1)), ("SVSV", "SVSV")
+BACK, BANKS, BW = ((0, 192, 0), (192, H, 96)), ((2, 3, 4, 5), (0, 1, 6, 7)), 320
+NVM = (5, 5)
+CYCLE, CALL, SETTLE, ISSUE, GATHER, SCATTER = 0.00088, 0.05, 0.18, 0.4, 1.56, 4.5
+ROUNDS, HASTE, OUT, PLAN = 3, 1.0, 0.003, {}
+PATIENCE = (0.05,)
+WAY = {"ma": 16.0, "mb": 16.0, "l0": 3.0, "mp": 8.0, "l1": 3.0, "k1": 6.0, "k2": 5.5, "k3": 5.0, "m2": 4.3, "m1": 4.3}
 F32, BF, U16, I32, FP4, U8, F16 = "float32", "bfloat16", "uint16", "int32", "float8_e4m3fn_x4", "uint8", "float16"
 
 
@@ -23,35 +33,37 @@ SCRATCH = {
     "xt": _sb(4 * C, BF), "ut": _sb(512, BF), "vt": _sb(512, BF),
     "qx": _sb(C, FP4), "sx": _sb(C, U8), "qu": _sb(128, FP4), "su": _sb(128, U8), "qr": _sb(128, FP4), "sr": _sb(128, U8),
     "qv": _sb(128, FP4), "sv": _sb(128, U8), "qw": _sb(512, FP4), "sw": _sb(512, U8),
-    "et": _sb(2048, BF), "qe": _sb(512, FP4), "se": _sb(512, U8), "ones": _sb(128, BF), "idn": _sb(128, BF),
+    "et": _sb(2048, BF), "qe": _sb(512, FP4), "se": _sb(512, U8), "ones": _sb(C, BF), "idn": _sb(128, BF),
     "pc": _sb(1, I32), "ci": _sb(2, I32), "cf": _sb(16, F32), "tm": _sb(464, BF), "jrow": _sb(C, F32),
     "mask": _sb(464, BF), "nmask": _sb(C, BF), "cdg": _sb(H, BF), "cd1": _sb(32, BF), "cd2": _sb(32, BF),
     "c32": _sb(C, BF), "c16": _sb(H, BF), "idr": _sb(H, BF),
-    "iot": _sb(128, F32), "uoff": _sb(8, U16), "coff": _sb(112, U16),
+    "iot": _sb(128, F32), "uoff": _sb(8, U16), "coff": _sb(144, U16),
     "row0": _sb(C, F32), "row1": _sb(H, F32), "row2": _sb(H, F32), "mm": _sb(C, F32),
     "hold0": _sb(C, F32), "hold1": _sb(H, F32), "hold2": _sb(H, F32), "eq": _sb(C, BF), "eup": _sb(C, BF),
     "fl": _sb(20 * C, BF), "sc": _sb(20 * H, F16), "sg": _sb(14 * C, BF),
-    "sm": _sb(512, F32), "of": _sb(384, U16), "si": _sb(192, I32),
+    "sm": _sb(640, F32), "of": _sb(448, U16), "si": _sb(192, I32),
     "g0": _sb(C, F32), "g1": _sb(672, BF), "g2": _sb(496, BF), "dg": _sb(C, F32), "dgb": _sb(5 * C, BF),
     "cum": _sb(C, F16), "dgc": _sb(C, F16),
-    "srow": _sb(512, F32), "shold": _sb(C, F32), "srtw": _sb(32, F32), "sig1": _sb(C, F32), "sig2": _sb(H, F32),
+    "xv": _sb(8 * C, BF), "xs": _sb(8 * 336, BF), "cs": _sb(8 * H + 16, BF), "cg": _sb(C, BF), "ct": _sb(C, BF), "cu": _sb(C, BF),
+    "cbig": _sb(464, BF),
+    "srow": _sb(512, F32), "shold": _sb(480, F32), "sig1": _sb(C, F32), "sig2": _sb(H, F32),
     "pdup": _sb(C, F32), "f1": _sb(C, BF), "f1s": _sb(C, BF), "f2": _sb(C, BF), "f2t": _sb(C, BF), "f2s": _sb(C, BF),
     "at1": _sb(HW, BF), "at2": _sb(HW, BF), "ag1": _sb(C, BF), "ag2": _sb(C, BF),
     "tph": _sb(4 * C, BF), "t8": _sb(4 * C, BF), "hp": _sb(4 * HW, BF), "ho": _sb(4 * OW, BF), "ztmp": _sb(4 * H, BF),
     "z1": _sb(4 * H, BF), "z2": _sb(4 * H, BF), "p1": _sb(4 * H, BF), "p2": _sb(4 * H, BF), "e2": _sb(4 * H, BF),
-    "b2": _sb(4 * H, BF), "b1": _sb(4 * H, BF), "xf": _sb(4 * C, BF), "y2": _sb(4 * C, BF), "y1": _sb(4 * C, BF),
+    "b2": _sb(4 * BW, BF), "b1": _sb(4 * BW, BF), "xf": _sb(4 * C, BF), "y2": _sb(4 * C, BF), "y1": _sb(4 * C, BF),
     "v8": _sb(4 * VW, BF), "d1": _sb(4 * VW, BF), "d0": _sb(4 * VW, BF),
-    "qa": _sb(3 * H, FP4), "sa": _sb(3 * H, U8), "qp1": _sb(H, FP4), "sp1": _sb(H, U8), "qp2": _sb(H, FP4), "sp2": _sb(H, U8),
-    "qb2": _sb(H, FP4), "sb2": _sb(H, U8), "qb1": _sb(H, FP4), "sb1": _sb(H, U8), "qo": _sb(C, FP4), "so": _sb(C, U8),
+    "qa": _sb(4 * H, FP4), "sa": _sb(4 * H, U8), "qp1": _sb(H, FP4), "sp1": _sb(H, U8), "qp2": _sb(H, FP4), "sp2": _sb(H, U8),
+    "qb2": _sb(BW, FP4), "sb2": _sb(BW, U8), "qb1": _sb(BW, FP4), "sb1": _sb(BW, U8), "qo": _sb(C, FP4), "so": _sb(C, U8),
     "rq": _sb(C + 3 * H, FP4), "rs": _sb(C + 3 * H, U8), "lq": _sb(C + 3 * H, FP4), "ls": _sb(C + 3 * H, U8),
     "rl": _sb(112, U16), "ll": _sb(112, U16),
     "mr": _sb(3 * VW, BF), "ix": _sb(2 * C, BF), "un": _sb(5 * C, BF), "ucr": _sb(C, F32), "yo": _sb(C, F32),
 }
-MSGS = ["mx", "l0", "mp", "l1", "k1", "k2", "m2", "m1"]
-SEMAPHORES = (["cV", "cS", "cT", "cG", "lsent", "a_k3"] + ["r_" + m for m in MSGS] + ["a_" + m for m in MSGS] + ["r_mx2"]
+MSGS = ["ma", "mb", "l0", "mp", "l1", "k1", "k2", "m2", "m1"]
+SEMAPHORES = (["cV", "cS", "cT", "cG", "lsent", "a_k3"] + ["r_" + m for m in MSGS] + ["a_" + m for m in MSGS]
               + ["d%d" % i for i in range(24)])
-BASE = {"mx": 0, "mp": C, "m2": C + H, "m1": C + 2 * H, "l0": 0, "l1": 32, "k1": 64, "k2": 80, "k3": 96}
-FORWARD = ("mx", "l0", "mp", "l1")
+BASE = {"ma": 0, "mb": H, "mp": C, "m2": C + H, "m1": C + 2 * H, "l0": 0, "l1": 32, "k1": 64, "k2": 80, "k3": 96}
+FORWARD = ("ma", "mb", "l0", "mp", "l1")
 
 
 def R(name, lo, hi, step=1):
@@ -63,13 +75,24 @@ def bank(b, n, lo=0):
 
 
 def pieces(msg):
-    if msg == "mx":
-        return [[(i, "q", 112 * i, 112 * i + 112, "r_mx") for i in range(4)], [(1, "s", 0, C, "r_mx2")]]
-    if msg in ("mp", "m2", "m1"):
+    if msg == "ma":
+        return [[(i, "q", 56 * i, 56 * i + 56, "r_ma") for i in range(4)]]
+    if msg == "mb":
+        return [[(1, "q", 0, 112, "r_mb"), (3, "q", 112, H, "r_mb"), (2, "s", -H, H, "r_mb")]]
+    if msg in ("m2", "m1"):
+        return [[(0, "q", 0, 84, "r_" + msg), (2, "q", 84, 168, "r_" + msg)], [(1, "q", 168, H, "r_" + msg), (3, "s", 0, H, "r_" + msg)]]
+    if msg == "mp":
         return [[(0, "q", 0, 112, "r_" + msg), (2, "q", 112, H, "r_" + msg)], [(1, "s", 0, H, "r_" + msg)]]
     if msg in ("l0", "l1"):
         return [[(0, "l", 0, 28, "r_" + msg)]]
     return [[(3, "l", 0, 14, "r_" + msg)]]
+
+
+def share(engines, call):
+    per = 1
+    while 2 * per * len(call) <= len(engines):
+        per *= 2
+    return per
 
 
 def relays_of(rank_core, far, topo):
@@ -108,7 +131,7 @@ def relay_program(g, core, T, topo):
             for (i, kind, lo, hi, sem) in call:
                 if i != me:
                     continue
-                g.wait_ge(T.sem[sem], len(topo.engines(owner[0], core)) // len(call))
+                g.wait_ge(T.sem[sem], share(topo.engines(owner[0], core), call))
                 rid, pid = topo.addr(dst, core)
                 b = BASE[msg]
                 g.remote_dma(side(T, kind, "l", b + lo, b + hi), side(T, kind, "r", b + lo, b + hi), T.sem["a_" + msg], T.sem.lsent,
@@ -118,7 +141,7 @@ def relay_program(g, core, T, topo):
 
 
 def make_builder(g, T):
-    ops, acc, sent = [], {}, [0]
+    ops, acc, sent, head, gate = [], {}, [0], [], [None]
     Q = {"V": g.vector, "S": g.scalar, "T": g.tensor, "G": g, "Y": g.sync}
     ndma = [0]
 
@@ -127,7 +150,7 @@ def make_builder(g, T):
             return {r[1] // 512}
         return set(range(r[1], r[2], r[3]))
 
-    def add(q, fn, reads, writes, dma=False, remote=False):
+    def add(q, fn, reads, writes, busy, dma=0.0, remote=None):
         i = len(ops)
         deps = set()
         for r, w in [(r, False) for r in reads] + [(r, True) for r in writes]:
@@ -141,27 +164,111 @@ def make_builder(g, T):
         if dma:
             tok = ("d%d" % ndma[0], 16)
             ndma[0] += 1
-        ops.append({"q": q, "fn": fn, "deps": deps, "tok": tok, "need": dma, "plain": not (dma or remote)})
+        ops.append({"q": q, "fn": fn, "deps": deps, "tok": tok, "need": bool(dma), "plain": not (dma or remote), "busy": busy,
+                    "done": dma or busy + SETTLE, "msg": remote, "behind": gate[0]})
         return i
 
-    def arrival(sem, val, writes):
-        i = add(None, None, [], writes, remote=True)
-        ops[i]["tok"] = (sem, val)
+    def aside(on):
+        gate[0] = len(ops) - 1 if on else None
+
+    def arrival(msg, val, writes, way):
+        i = add(None, None, [], writes, 0.0, remote=msg)
+        ops[i]["tok"] = ("a_" + msg, val)
+        ops[i]["done"] = way
+
+    def mark():
+        head.append(len(ops))
+
+    def arrange():
+        before = [set(o["deps"]) for o in ops]
+        lead = [{} for o in ops]
+        prev = {}
+        for i, o in enumerate(ops):
+            if o["q"] is None:
+                lead[i] = {j: 0.0 for j, p in enumerate(ops) if p["q"] == "G" and p["msg"] == o["msg"]}
+            elif not o["plain"] or o["q"] == "G":
+                if o["q"] in prev:
+                    lead[i] = {prev[o["q"]]: ops[prev[o["q"]]]["busy"]}
+                prev[o["q"]] = i
+            if o["behind"] is not None and o["q"] == "V":
+                lead[i].setdefault(o["behind"], 0.0)
+        edge = [{**lead[i], **{d: ops[d]["done"] for d in before[i]}} for i in range(len(ops))]
+        back = [{} for o in ops]
+        for i, e in enumerate(edge):
+            for d, w in e.items():
+                back[d][i] = w * (HASTE if ops[d]["q"] is None else 1.0) - ops[d]["busy"] + ops[i]["busy"]
+
+        def fit(order, edges, first):
+            at, taken = {}, {q: [] for q in Q}
+            for i in order:
+                t = max([first(i)] + [at[d] + w + 1e-6 for d, w in edges[i].items()])
+                q, busy = ops[i]["q"], ops[i]["busy"]
+                if q is not None:
+                    for (a, b) in taken[q]:
+                        if t + busy <= a:
+                            break
+                        t = max(t, b)
+                    taken[q].append((t, t + busy))
+                    taken[q].sort()
+                at[i] = t
+            return at
+
+        def step(edges, follow, first, rank_, patience):
+            at, free, left = {}, {q: 0.0 for q in list(Q) + [None]}, [len(e) for e in edges]
+            ready = {i: first(i) for i in range(len(ops)) if not left[i]}
+            while ready:
+                soon = min(ready, key=lambda i: max(ready[i], free[ops[i]["q"]]))
+                q = ops[soon]["q"]
+                t0 = max(ready[soon], free[q])
+                i = min((j for j in ready if ops[j]["q"] == q and ready[j] <= t0 + patience), key=rank_)
+                at[i] = max(ready.pop(i), free[q])
+                if q is not None:
+                    free[q] = at[i] + ops[i]["busy"]
+                for j in follow[i]:
+                    left[j] -= 1
+                    if not left[j]:
+                        ready[j] = max([first(j)] + [at[d] + w + 1e-6 for d, w in edges[j].items()])
+            return at
+
+        def urgency(late):
+            return lambda i: (0, i) if head[0] <= i < head[1] else (1, -late[i] - ops[i]["busy"])
+
+        def tail(i):
+            return ops[i]["done"] - ops[i]["busy"]
+
+        best = PLAN.get(len(ops))
+        for patience in () if best else PATIENCE:
+            order = sorted(range(len(ops)), key=lambda i: max(lead[i]) + 0.5 if ops[i]["q"] is None else i)
+            at = fit(order, edge, lambda i: 0.0)
+            for _ in range(ROUNDS):
+                if patience is None:
+                    late = fit(sorted(at, key=lambda i: -at[i]), back, tail)
+                    at = fit(sorted(late, key=urgency(late)), edge, lambda i: 0.0)
+                else:
+                    late = step(back, edge, tail, lambda i: -at[i], patience)
+                    at = step(edge, back, lambda i: 0.0, urgency(late), patience)
+                end = max(at[i] + ops[i]["done"] for i in at)
+                if best is None or end < best[0]:
+                    best = (end, at, patience)
+        PLAN[len(ops)] = best
+        for i, t in best[1].items():
+            ops[i]["at"] = t
+        new = sorted(range(len(ops)), key=lambda i: ops[i]["at"])
+        place = {i: p for p, i in enumerate(new)}
+        ops[:] = [ops[i] for i in new]
+        for o in ops:
+            o["deps"] = {place[d] for d in o["deps"]}
 
     def emit():
-        hist = {q: [] for q in Q}
+        arrange()
         for i, o in enumerate(ops):
             last = {}
             for d in o["deps"]:
                 if ops[d]["tok"] is None:
                     last[ops[d]["q"]] = max(last.get(ops[d]["q"], -1), d)
-            q = o["q"]
-            if q in last and len(hist[q]) >= 3:
-                last[q] = max(last[q], hist[q][-3])
             o["deps"] = [d for d in o["deps"] if ops[d]["tok"] is not None] + list(last.values())
-            if q is not None and o["plain"]:
-                hist[q].append(i)
         seen = {q: {} for q in Q}
+        hist = {q: [] for q in Q}
         for i, o in enumerate(ops):
             if o["q"] is None:
                 o["clock"] = {("t", i): 1}
@@ -172,6 +279,8 @@ def make_builder(g, T):
                 key, val = (("t", d), 1) if ops[d]["tok"] is not None else (ops[d]["q"], d)
                 if k.get(key, -1) >= val:
                     continue
+                if key == o["q"]:
+                    d = max([d] + [j for j in hist[key][-12:] if ops[j]["at"] + ops[j]["done"] + 2 * SETTLE <= o["at"]])
                 keep.append(d)
                 ops[d]["need"] = True
                 for kk, vv in ops[d]["clock"].items():
@@ -183,6 +292,8 @@ def make_builder(g, T):
                 o["clock"][("t", i)] = 1
             else:
                 o["clock"][o["q"]] = i
+            if o["plain"]:
+                hist[o["q"]].append(i)
         count = {q: 0 for q in Q}
         for o in ops:
             if o["q"] is not None and o["tok"] is None and o["need"]:
@@ -204,7 +315,7 @@ def make_builder(g, T):
         for s, v in final.items():
             g.wait_ge(T.sem[s], v)
 
-    return add, arrival, emit, sent
+    return add, arrival, mark, aside, emit, sent
 
 
 def rank_program(g, core, T, topo):
@@ -215,7 +326,7 @@ def rank_program(g, core, T, topo):
     n = len(T.cores)
     nxt, prv2 = T.cores[(rank + 1) % n], T.cores[(rank - 2) % n]
     rel = relays_of(core, nxt, topo)
-    add, arrival, emit, sent = make_builder(g, T)
+    add, arrival, mark, aside, emit, sent = make_builder(g, T)
 
     def ap(r):
         if len(r) == 2:
@@ -232,26 +343,40 @@ def rank_program(g, core, T, topo):
     def val(s):
         return ap(s) if isinstance(s, tuple) else s
 
+    def size(r):
+        return 16 * size(r[1]) if len(r) == 2 else len(range(r[1], r[2], r[3]))
+
+    def span(out, *ins, slow=None):
+        if len(out) == 2:
+            return CALL + size(out) * SCATTER * CYCLE
+        if len(ins[0]) == 2:
+            return CALL + size(out) * GATHER * CYCLE
+        narrow = all(SCRATCH[r[0]][2] in (BF, F16, U16) for r in (out,) + ins)
+        return CALL / 2 + max(64, size(out) * (slow or (0.5 if narrow else 1.0))) * CYCLE
+
     def ts(out, a, s1, op0, s2=None, op1=None):
         if op1 is None:
-            add("V", lambda q: q.tensor_scalar(ap(out), ap(a), val(s1), None, op0), rd(a, s1), [out])
+            add("V", lambda q: q.tensor_scalar(ap(out), ap(a), val(s1), None, op0), rd(a, s1), [out], span(out, a))
         else:
-            add("V", lambda q: q.tensor_scalar(ap(out), ap(a), val(s1), val(s2), op0, op1), rd(a, s1, s2), [out])
+            add("V", lambda q: q.tensor_scalar(ap(out), ap(a), val(s1), val(s2), op0, op1), rd(a, s1, s2), [out], span(out, a))
 
     def tt(out, a, b, op):
-        add("V", lambda q: q.tensor_tensor(ap(out), ap(a), ap(b), op), rd(a, b), [out])
+        add("V", lambda q: q.tensor_tensor(ap(out), ap(a), ap(b), op), rd(a, b), [out], span(out, a, b, slow=1.0 if a[0] == "ps" else 2.0))
 
     def cp(out, a):
         if len(out) == 2:
-            add("V", lambda q: q.tensor_copy(ap(out), ap(a)), rd(a, out[1]), [out[0]])
+            add("V", lambda q: q.tensor_copy(ap(out), ap(a)), rd(a, out[1]), [out[0]], span(out, a))
         else:
-            add("V", lambda q: q.tensor_copy(ap(out), ap(a)), rd(a), [out])
+            add("V", lambda q: q.tensor_copy(ap(out), ap(a)), rd(a), [out], span(out, a))
 
     def scan(out, a, b, init, op0, op1):
-        add("V", lambda q: q.tensor_tensor_scan(ap(out), ap(a), ap(b), val(init), op0, op1), rd(a, b, init), [out])
+        add("V", lambda q: q.tensor_tensor_scan(ap(out), ap(a), ap(b), val(init), op0, op1), rd(a, b, init), [out], span(out, a, b))
+
+    def turn(out, a):
+        add("V", lambda q: q.transpose(ap(out), ap(a)), [a], [out], span(out, a))
 
     def mset(out, v):
-        add("V", lambda q: q.memset(ap(out), v), [], [out])
+        add("V", lambda q: q.memset(ap(out), v), [], [out], span(out, out))
 
     def act(out, a, f=AF.Copy, bias=None, scale=None, accum=None):
         kw = {}
@@ -261,11 +386,12 @@ def rank_program(g, core, T, topo):
             kw["scale"] = val(scale)
         if accum is not None:
             kw["accum_out"] = ap(accum)
-        add("S", lambda q: q.activation(ap(out), ap(a), f, **kw), rd(a, bias, scale), [out] + rd(accum))
+        add("S", lambda q: q.activation(ap(out), ap(a), f, **kw), rd(a, bias, scale), [out] + rd(accum),
+            span(out, a, slow=1.0) + CALL / 2 + (0.02 if accum else 0.0))
 
     def fill(out, v):
         m = len(range(out[1], out[2], out[3]))
-        act(out, R("tm", 0, m), AF.Identity, v, 0.0)
+        act(out, R("ones", 0, m), AF.Identity, v, 0.0)
 
     def mov(e, out, a, k=None):
         if e == "S":
@@ -276,10 +402,11 @@ def rank_program(g, core, T, topo):
             ts(out, a, k, OP.mult)
 
     def quant(q_, s_, a):
-        add("V", lambda q: q.quantize_mx(ap(q_), ap(s_), ap(a)), [a], [q_, s_])
+        add("V", lambda q: q.quantize_mx(ap(q_), ap(s_), ap(a)), [a], [q_, s_], 0.012 + 0.00022 * size(a))
 
     def mm(out, lq, ls, rq, rs):
-        add("T", lambda q: q.matmul_mx(ap(out), ap(lq), ap(ls), ap(rq), ap(rs), True, True), [lq, ls, rq, rs], [out])
+        add("T", lambda q: q.matmul_mx(ap(out), ap(lq), ap(ls), ap(rq), ap(rs), True, True), [lq, ls, rq, rs], [out],
+            (size(rq) + 16) * 0.0006)
 
     def four(w, q_, s_, m, b0=2):
         for b in range(4):
@@ -287,15 +414,15 @@ def rank_program(g, core, T, topo):
 
     def iota(out, pat, base, cm=0):
         kw = {} if out[0] == "pc" else {"allow_small_or_imprecise_dtypes": True}
-        add("G", lambda q: q.iota(ap(out), pat, base, cm, **kw), [], [out])
+        add("G", lambda q: q.iota(ap(out), pat, base, cm, **kw), [], [out], 0.13 + 2.4 * size(out) * CYCLE)
 
-    def dma(e, out, in_, reads, writes):
-        add(e, lambda q: q.dma_start(out, in_), reads, writes, dma=True)
+    def dma(e, out, in_, reads, writes, way):
+        add(e, lambda q: q.dma_start(out, in_), reads, writes, CALL, dma=way)
 
     def send(msg, src):
         for call in pieces(msg):
             eng = topo.engines(core, rel[0])
-            per = len(eng) // len(call)
+            per = share(eng, call)
             trs, reads = [], []
             for j, (i, kind, lo, hi, sem) in enumerate(call):
                 name, b0 = src[kind]
@@ -307,17 +434,18 @@ def rank_program(g, core, T, topo):
             sent[0] += per * len(call)
             if len(trs) == 1:
                 t = trs[0]
-                add("G", lambda q, t=t: q.remote_dma(t[1], t[0], t[2], T.sem.lsent, t[3], t[4], t[5]), reads, [], remote=True)
+                add("G", lambda q, t=t: q.remote_dma(t[1], t[0], t[2], T.sem.lsent, t[3], t[4], t[5]), reads, [], ISSUE, remote=msg)
             else:
                 add("G", lambda q, trs=trs: q.remote_dma_fused(
                     [RemoteDMATransfer(dst_ids=[DstId(rid=t[4], pnc=t[3])], dma_engine_mask=t[5], remote_sem=t[2], src=t[0], dst=t[1])
-                     for t in trs], local_sem=T.sem.lsent), reads, [], remote=True)
+                     for t in trs], local_sem=T.sem.lsent), reads, [], ISSUE, remote=msg)
 
     far = len(topo.engines(rel[0], nxt))
     for msg in MSGS:
         ps_ = [p for call in pieces(msg) for p in call]
-        arrival("a_" + msg, far * len(ps_), [R("l" + k, BASE[msg] + lo, BASE[msg] + hi) for (i, k, lo, hi, s) in ps_])
-    arrival("a_k3", len(topo.engines(T.cores[(rank + 2) % n], core)), [R("ll", BASE["k3"], BASE["k3"] + 14)])
+        arrival(msg, far * len(ps_), [R("l" + k, BASE[msg] + lo, BASE[msg] + hi) for (i, k, lo, hi, s) in ps_],
+                WAY[msg])
+    arrival("k3", len(topo.engines(T.cores[(rank + 2) % n], core)), [R("ll", BASE["k3"], BASE["k3"] + 14)], WAY["k3"])
 
     def col(j):
         return R("cf", j, j + 1)
@@ -341,100 +469,198 @@ def rank_program(g, core, T, topo):
     def word(name, t, lo, hi):
         return R(name, 4 * lo + t, 4 * hi, 4)
 
-    dma("S", T.ut[:], T.u[:], [], [R("ut", 0, 512)])
+    mark()
+    dma("S", T.ut[:], T.u[:], [], [R("ut", 0, 512)], 1.9)
     for j in range(2):
-        dma("Y", T.xt[:, 4 * H * j:4 * H * j + 4 * H], T.x[:, 4 * H * j:4 * H * j + 4 * H], [], [R("xt", 4 * H * j, 4 * H * j + 4 * H)])
+        dma("Y", T.xt[:, 4 * H * j:4 * H * j + 4 * H], T.x[:, 4 * H * j:4 * H * j + 4 * H], [], [R("xt", 4 * H * j, 4 * H * j + 4 * H)],
+            2.8 + 0.9 * j)
     iota(R("pc", 0, 1), [[0, 1]], 0, 1)
-    mset(R("ones", 0, 128), 1.0)
+    mset(R("ones", 0, C), 1.0)
     mset(R("et", 0, 2048), 0.0)
-    add("G", lambda q: q.affine_select(T.idn[:], T.ones[:], [[-1, 128]], OP.is_equal, 0.0, 0, 1), [R("ones", 0, 128)], [R("idn", 0, 128)])
-    iota(R("tm", 0, 464), [[0, 29], [1, 16]], 0)
+    fill(R("c32", 0, C), 1.0)
+    for nm in ("xv", "xs"):
+        fill(R(nm, 7, 8 * H, 8), DROP)
+    fill(R("cs", 0, 8), 0.0)
+    fill(R("srow", C, 512), BIG)
+    fill(R("c32", 0, C, 32), 0.0)
+    for nm, w in (("hp", HW), ("ho", OW)):
+        fill(R(nm, 0, 4 * w, w), 0.0)
     iota(R("iot", 0, 8), [[16, 8]], 0)
+    iota(R("tm", 0, 464), [[0, 29], [1, 16]], 0)
+    add("G", lambda q: q.affine_select(T.idn[:], T.ones[:, 0:128], [[-1, 128]], OP.is_equal, 0.0, 0, 1), [R("ones", 0, 128)], [R("idn", 0, 128)], 0.45)
     iota(R("iot", 78, 106), [[16, 28]], 16)
+    iota(R("iot", 106, 120), [[128, 14]], 14)
     iota(R("iot", 8, 36), [[16, 14], [0, 2]], 15)
     iota(R("iot", 36, 50), [[16, 14]], 15)
     iota(R("iot", 50, 78), [[0, 14], [256, 2]], 15)
     iota(R("jrow", 0, C), [[1, C]], 1)
     ts(R("ci", 0, 1), R("pc", 0, 1), 15, OP.bitwise_and)
     ts(R("ci", 1, 2), R("pc", 0, 1), 4, OP.logical_shift_right, 1, OP.bitwise_and)
+    cp(R("uoff", 0, 8), R("iot", 0, 8))
     cp(R("cf", 0, 2), R("ci", 0, 2))
-    for b in range(4):
-        act(R("et", 512 * b + b, 512 * b + 512, 4), R("idn", 0, 128))
-    quant(R("qe", 0, 512), R("se", 0, 512), R("et", 0, 2048))
     ts(R("mask", 0, 464), R("tm", 0, 464), col(0), OP.is_equal)
     ts(R("nmask", 0, C), R("tm", 0, C), col(0), OP.not_equal)
-    cp(R("uoff", 0, 8), R("iot", 0, 8))
-    act(R("cd1", 0, 32), R("mask", 15, 47), AF.Identity, 1.0, -(1.0 - SH))
-    act(R("cd2", 0, 32), R("mask", 16, 48), AF.Copy, None, 2.0 ** 60)
     quant(R("qu", 0, 128), R("su", 0, 128), R("ut", 0, 512))
     add("V", lambda q: q.tensor_copy(T.qr[:, 0:128].bitcast(dt.uint32), T.qu[:, 0:128].bitcast(dt.uint32).indirect(T.uoff[:, 0:8])),
-        [R("qu", 0, 128), R("uoff", 0, 8)], [R("qr", 0, 128)])
+        [R("qu", 0, 128), R("uoff", 0, 8)], [R("qr", 0, 128)], 0.23)
     add("S", lambda q: q.activation(T.sr[:, 0:128], T.su[:, 0:128].indirect(T.uoff[:, 0:8]), AF.Copy),
-        [R("su", 0, 128), R("uoff", 0, 8)], [R("sr", 0, 128)])
-    tt(R("cdg", 0, 32), R("cd1", 0, 32), R("cd2", 0, 32), OP.max)
-    for lo, hi in ((32, 64), (64, 128), (128, H)):
-        act(R("cdg", lo, hi), R("cdg", 0, hi - lo))
-    act(col(3), R("mask", 15, 16), AF.Identity, 1.0 / SH, 1.0 - 1.0 / SH)
-    dma("Y", T.qw[:].bitcast(dt.uint8), T.wc[:], [R("xt", 4 * C - 1, 4 * C)], [R("qw", 0, 512)])
-    dma("Y", T.sw[:], T.ws[:], [], [R("sw", 0, 512)])
-    dma("Y", T.vt[:], T.v[:], [], [R("vt", 0, 512)])
+        [R("su", 0, 128), R("uoff", 0, 8)], [R("sr", 0, 128)], 0.25)
+    x1, x2, xd, xs1, xs2 = R("coff", 0, 28), R("coff", 28, 42), R("coff", 42, 70), R("coff", 70, 98), R("coff", 98, 112)
+    xc = R("coff", 112, 140)
     qr, sr = R("qr", 0, 128), R("sr", 0, 128)
-    for j in range(2):
-        quant(R("qx", H * j, H * j + H), R("sx", H * j, H * j + H), R("xt", 4 * H * j, 4 * H * j + 4 * H))
-        for b in (6 * j, 6 * j + 1):
-            mm(bank(b, H), qr, sr, R("qx", H * j, H * j + H), R("sx", H * j, H * j + H))
-    send("mx", {"q": ("qx", 0), "s": ("sx", 0)})
 
-    def ranks(m, parts, row, hold, nv, between, win, ids):
-        nk, h = m // 16, m // 2
-        ns = nk - nv
-        vs, ss = list(range(ns, nk)), list(range(ns))
-        for i, (b_v, b_s) in enumerate(parts):
-            act(R(row, H * i, H * i + H), bank(b_s, H))
-            tt(R("mm", H * i, H * i + H), bank(b_v, H), R("mask", 16, 16 + H), OP.mult)
-            if i == 1:
-                tt(R("eq", 0, H), bank(parts[0][0], H), R(hold, 0, H), OP.is_equal)
-            scan(R(hold, H * i, H * i + H), R("nmask", 0, H), R("mm", H * i, H * i + H), 0.0, OP.mult, OP.add)
-        lt, gt, init, base, dif, out, off = sm(nk), sm(nk), sm(nk), sm(nk), sm(nk), sm(nk), of(nk)
-        between.get("S0", lambda: None)()
-        for j, k in enumerate(ss):
-            act(R("sg", m * j, m * j + m), R(row, 0, m), AF.Sign, R(hold, 16 * k + 15, 16 * k + 16), -1.0)
-        for j, k in enumerate(ss):
-            lo, hi = R("sg", m * j, m * j + 16 * k + 16), R("sg", m * j + 16 * k + 16, m * j + m)
-            act(lo, lo, AF.Relu, None, -1.0, sub(gt, k, k + 1))
-            act(hi, hi, AF.Relu, None, None, sub(lt, k, k + 1))
-        between.get("V0", lambda i: None)(init)
-        tt(R("eq", m - H, m), bank(parts[-1][0], H), R(hold, m - H, m), OP.is_equal)
-        for j, k in enumerate(vs):
-            s, e = R(hold, 16 * k + 15, 16 * k + 16), 16 * k + 16
-            ts(R("fl", m * j, m * j + e), R(row, 0, e), s, OP.is_le)
+    def constants():
+        for b in range(4):
+            act(R("et", 512 * b + b, 512 * b + 512, 4), R("idn", 0, 128))
+        act(col(4), col(0), AF.Copy, None, 16.0)
+        act(col(5), col(1), AF.Copy, None, 448.0)
+        act(col(6), col(1), AF.Identity, 448.0, -448.0)
+        act(col(7), col(0), AF.Copy, None, 8.0)
+        for j in range(2):
+            quant(R("qe", 256 * j, 256 * j + 256), R("se", 256 * j, 256 * j + 256), R("et", 1024 * j, 1024 * j + 1024))
+        act(R("cd1", 0, 32), R("mask", 15, 47), AF.Identity, 1.0, -(1.0 - SH))
+        act(R("cd2", 0, 32), R("mask", 16, 48), AF.Copy, None, 2.0 ** 60)
+        act(col(8), col(1), AF.Identity, col(7), -4096.0)
+        act(col(9), col(6), AF.Identity, col(7), -16.0)
+        act(col(3), R("mask", 15, 16), AF.Identity, 1.0 / SH, 1.0 - 1.0 / SH)
+        tt(R("cdg", 0, 32), R("cd1", 0, 32), R("cd2", 0, 32), OP.max)
+        for lo, hi in ((32, 64), (64, 128), (128, H)):
+            act(R("cdg", lo, hi), R("cdg", 0, hi - lo))
+        ts(sub(xc, 0, 28, 2), R("iot", 106, 120), col(8), OP.add)
+        ts(sub(xc, 1, 28, 2), R("iot", 106, 120), col(9), OP.add)
+
+    def gfill(out, v):
+        iota(out, [[0, len(range(out[1], out[2], out[3]))]], v)
+
+    def first_ranks():
+        hk, hh = 14, H // 2
+        nsa = hk - NVA
+        a_s, a_v, b_s, b_v = list(range(nsa)), list(range(nsa, hk)), list(range(hk, hk + 7)), list(range(hk + 7, 2 * hk))
+        lt, gt, init, base, dif, pre, out = (sm(28) for _ in range(7))
+        o_a, o_bs, o_bv = of(hk), of(8), of(8)
+
+        def held(k):
+            return R("hold0", 16 * k + 15, 16 * k + 16)
+
+        def scores(j):
+            lo, hi = H * j, H * j + H
+            quant(R("qx", lo, hi), R("sx", lo, hi), R("xt", 4 * lo, 4 * hi))
+            for b in (6 * j, 6 * j + 1):
+                mm(bank(b, H), qr, sr, R("qx", lo, hi), R("sx", lo, hi))
+            send(("ma", "mb")[j], {"q": ("qx", lo), "s": ("sx", lo)})
+
+        def row(j):
+            act(R("row0", H * j, H * j + H), bank(6 * j + 1, H))
+
+        def masked(j):
+            tt(R("mm", H * j, H * j + H), bank(6 * j, H), R("mask", 0, H), OP.mult)
+
+        def hold(j):
+            scan(R("hold0", H * j, H * j + H), R("nmask", 0, H), R("mm", H * j, H * j + H), 0.0, OP.mult, OP.add)
+
+        def equal(j):
+            tt(R("eq", H * j, H * j + H), bank(6 * j, H), R("hold0", H * j, H * j + H), OP.is_equal)
+
+        def behind(j):
+            scan(R("eup", H * j, H * j + H), R("eq", H * j, H * j + H), R("nmask", 0, H), 0.0, OP.add, OP.mult)
+
+        def start(j):
+            ts(sub(init, hk * j, hk * j + hk), R("eup", H * j + 15, H * j + H, 16), -1.0, OP.mult, (111.0, -1.0)[j], OP.add)
+
+        def v_flags(k):
+            e, m = 16 * k + 16, H if k < hk else C
+            ts(flag(k, 0, e), R("row0", 0, e), held(k), OP.is_le)
             if e < m:
-                ts(R("fl", m * j + e, m * j + m), R(row, e, m), s, OP.is_lt)
-            if j == 0:
-                scan(R("eup", 0, m), R("eq", 0, m), R("nmask", 0, m), 0.0, OP.add, OP.mult)
-            between.get(("V", j), lambda i: None)(init)
-        once = len(parts) == 1
-        for j, k in enumerate(vs):
-            scan(R("sc", h * j, h * j + h), R("fl", m * j, m * j + h), R("fl", m * j + h, m * j + m), sub(init, k, k + 1), OP.add, OP.add)
-            if j == 0:
-                tt(sub(base, 0, ns), sub(init, 0, ns), R("iot", 78, 78 + ns), OP.add)
-            if once and j == nv - 2:
-                tt(sub(dif, 0, ns), sub(base, 0, ns), sub(gt, 0, ns), OP.subtract)
-        ends = R("sc", h - 1, h * nv, h)
-        if once:
-            tt(sub(out, 0, ns), sub(dif, 0, ns), sub(lt, 0, ns), OP.add)
-            cp(sub(off, ns, nk), ends)
-            cp(sub(off, 0, ns), sub(out, 0, ns))
-            cp((win, off), R(ids, 0, m))
-            return out, lambda: cp(sub(out, ns, nk), ends)
-        cp(sub(off, ns, nk), ends)
-        cp((win, sub(off, ns, nk)), R(ids, 16 * ns, m))
-        tt(sub(dif, 0, ns), sub(base, 0, ns), sub(gt, 0, ns), OP.subtract)
-        cp(sub(out, ns, nk), ends)
-        tt(sub(out, 0, ns), sub(dif, 0, ns), sub(lt, 0, ns), OP.add)
-        cp(sub(off, 0, ns), sub(out, 0, ns))
-        cp((win, sub(off, 0, ns)), R(ids, 0, 16 * ns))
-        return out, None
+                ts(flag(k, e, m), R("row0", e, m), held(k), OP.is_lt)
+
+        def flag(k, lo, hi):
+            return R("fl", H * k + lo, H * k + hi) if k < hk else R("xv", 8 * lo + k - b_v[0], 8 * hi, 8)
+
+        def v_sum(k):
+            h, s0 = (hh, hh * k) if k < hk else (H, H * (k - hk))
+            scan(R("sc", s0, s0 + h), flag(k, 0, h), flag(k, h, 2 * h), sub(init, k, k + 1), OP.add, OP.add)
+
+        def sg(k, lo, hi):
+            b0 = H * k if k < hk else H * nsa + C * (k - hk)
+            return R("sg", b0 + lo, b0 + hi)
+
+        def s_sign(k):
+            m = H if k < hk else 16 * k + 16
+            act(sg(k, 0, m), R("row0", 0, m), AF.Sign, held(k), -1.0)
+
+        def s_rest(k):
+            act(sg(k, 16 * k + 16, C), R("row0", 16 * k + 16, C), AF.Sign, held(k), -1.0)
+
+        def s_above(k):
+            e = 16 * k + 16
+            act(sg(k, 0, e) if k < hk else R("xs", k - hk, 8 * e, 8), sg(k, 0, e), AF.Relu, None, -1.0, sub(gt, k, k + 1))
+
+        def s_below(k):
+            e, m = 16 * k + 16, H if k < hk else C
+            act(sg(k, e, m), sg(k, e, m), AF.Relu, None, None, sub(lt, k, k + 1))
+
+        def each(f, ks):
+            for k in ks:
+                f(k)
+
+        scores(0)
+        row(0)
+        masked(0)
+        hold(0)
+        each(s_sign, a_s[:EARLY_S])
+        constants()
+        mark()
+        equal(0)
+        v_flags(a_v[0])
+        scores(1)
+        row(1)
+        each(s_sign, a_s[EARLY_S:])
+        behind(0)
+        each(v_flags, a_v[1:EARLY_V])
+        masked(1)
+        start(0)
+        hold(1)
+        each(s_sign, b_s)
+        each(s_above, b_s)
+        each(v_sum, a_v[:EARLY_V])
+        equal(1)
+        v_flags(b_v[0])
+        behind(1)
+        v_flags(b_v[1])
+        start(1)
+        each(v_flags, b_v[2:])
+        dma("Y", T.qw[:].bitcast(dt.uint8), T.wc[:], [R("xv", 6, 7)], [R("qw", 0, 512)], 8.0)
+        dma("Y", T.sw[:], T.ws[:], [], [R("sw", 0, 512)], 8.0)
+        dma("Y", T.vt[:], T.v[:], [], [R("vt", 0, 512)], 20.0)
+        each(v_sum, b_v)
+        each(v_flags, a_v[EARLY_V:EARLY_V + MID_V])
+        scan(R("cs", 8, 8 + 8 * H), R("xv", 0, 8 * H), R("xs", 0, 8 * H), 0.0, OP.add, OP.subtract)
+        each(s_above, a_s)
+        each(s_below, a_s[:MID_S])
+        act(R("cg", 0, C), (R("cs", 0, 8 + 8 * H), xc))
+        each(s_below, a_s[MID_S:])
+        each(s_rest, b_s)
+        each(s_below, b_s)
+        ends = R("sc", 8 * H - 1, 14 * H, H)
+        cp(sub(o_bv, 0, 7), ends)
+        tt(base, init, R("iot", 78, 106), OP.add)
+        each(v_flags, a_v[EARLY_V + MID_V:])
+        turn(R("ct", 0, C), R("cg", 0, C))
+        each(v_sum, a_v[EARLY_V:])
+        tt(sub(dif, 0, nsa), sub(base, 0, nsa), sub(gt, 0, nsa), OP.subtract)
+        scan(R("cu", 0, C), R("c32", 0, C), R("ct", 0, C), 0.0, OP.mult, OP.add)
+        cp(sub(pre, nsa, hk), R("sc", hh * nsa + hh - 1, hh * hk, hh))
+        tt(sub(pre, 0, nsa), sub(dif, 0, nsa), sub(lt, 0, nsa), OP.add)
+        tt(sub(dif, hk, hk + 7), sub(base, hk, hk + 7), sub(gt, hk, hk + 7), OP.subtract)
+        tt(sub(out, 0, hk), sub(pre, 0, hk), R("cu", 31, C, 32), OP.subtract)
+        cp((R("g0", 0, C), sub(o_bv, 0, 7)), R("jrow", 16 * b_v[0], C))
+        cp(o_a, sub(out, 0, hk))
+        tt(sub(out, hk, hk + 7), sub(dif, hk, hk + 7), sub(lt, hk, hk + 7), OP.add)
+        cp(sub(o_bs, 0, 7), sub(out, hk, hk + 7))
+        cp((R("g0", 0, C), o_a), R("jrow", 0, H))
+        cp((R("g0", 0, C), sub(o_bs, 0, 7)), R("jrow", H, 16 * b_v[0]))
+        cp(sub(out, b_v[0], 28), ends)
+        return out
 
     def diag(out, a):
         scan(out, R("cdg", 0, H), a, 1.0, OP.mult, OP.min)
@@ -455,151 +681,194 @@ def rank_program(g, core, T, topo):
         ts(o, i1, 224.0, OP.min)
         return o
 
-    r0, _ = ranks(C, [(0, 1), (6, 7)], "row0", "hold0", NV0,
-                  {("V", 2): lambda init: ts(init, R("eup", 15, C, 16), -1.0, OP.mult, -1.0, OP.add)}, R("g0", 0, C), "jrow")
-    four("e", R("lq", 0, C), R("ls", 0, C), C)
+    r0 = first_ranks()
+    act(R("cbig", 0, 464), R("mask", 0, 464), AF.Copy, None, BIG)
+    tb = (0, 1, 6, 7)
     for t in range(4):
-        act(plane("tph", C, t), bank(2 + t, C), AF.Copy, None, 0.5)
+        mm(bank(tb[t], C), R("qe", 128 * t, 128 * t + 128), R("se", 128 * t, 128 * t + 128), R("qx", 0, C), R("sx", 0, C))
+    act(R("idr", 0, H), R("jrow", 0, H), AF.Copy, None, 2.0 ** -17)
     diag(R("dg", 0, H), R("g0", 0, C, 2))
     diag(R("dg", H, C), R("g0", 1, C, 2))
     l0 = of(28)
     ts(l0, R("dg", 15, C, 16), col(3), OP.mult, -1.0, OP.add)
+    aside(True)
+    for t in range(4):
+        mov("SSVV"[t], plane("t8", C, t), bank(tb[t], C), 0.125)
+    aside(False)
     send("l0", {"l": ("of", l0[1])})
-    four("e", R("qx", 0, C), R("sx", 0, C), C)
-    mset(R("srow", C, 512), BIG)
-    cp(R("srow", 0, C, 2), (R("row0", 0, C), sub(l0, 0, 14)))
-    cp(R("srow", 1, C, 2), (R("row0", 0, C), sub(l0, 14, 28)))
-    act(col(4), col(0), AF.Copy, None, 16.0)
-    act(col(5), col(1), AF.Copy, None, 28.0)
-    act(col(6), col(1), AF.Identity, 28.0, -28.0)
-    fill(R("hp", 0, 4 * HW, HW), 0.0)
-    act(R("idr", 0, H), R("jrow", 0, H), AF.Copy, None, 2.0 ** -17)
-    mset(R("srtw", 28, 32), BIG)
-    mset(R("c32", 0, C), 1.0)
-    tt(R("mm", 0, C), R("srow", 0, C), R("mask", 16, 16 + C), OP.mult)
-    x1, x2, xd, xs1, xs2 = R("coff", 0, 28), R("coff", 28, 42), R("coff", 42, 70), R("coff", 70, 98), R("coff", 98, 112)
     cp(R("coff", 0, 42), R("iot", 8, 50))
     ts(xd, R("iot", 8, 36), col(0), OP.add, -15.0, OP.add)
     ts(xs1, R("iot", 50, 78), col(4), OP.add)
     ts(xs2, R("iot", 50, 78, 2), col(4), OP.add)
-    scan(R("shold", 0, C), R("nmask", 0, C), R("mm", 0, C), 0.0, OP.mult, OP.add)
-    fill(R("c32", 0, C, 32), 0.0)
-    act(R("sig1", 0, C), (R("srow", 0, 512), xs1))
-    for t in range(4):
-        act(plane("t8", C, t), bank(2 + t, C), AF.Copy, None, 0.125)
-    mset(R("g1", 0, 672), 1.0)
-    cp(R("srtw", 0, 28), R("shold", 15, C, 16))
-    mset(R("at1", 0, HW), 225.0)
+    gfill(R("g1", 0, 672), 1)
+    gfill(R("at1", 0, HW), 225)
+    cp(R("srow", 0, C, 2), (R("row0", 0, C), sub(l0, 0, 14)))
+    cp(R("srow", 1, C, 2), (R("row0", 0, C), sub(l0, 14, 28)))
     o_r = of(28)
     ts(o_r, r0, 225.0, OP.add)
-    o_x0 = halved(r0, 28)
-    quant(R("qv", 0, 128), R("sv", 0, 128), R("vt", 0, 512))
+    scan(R("shold", 1, 465), R("cbig", 0, 464), R("srow", 0, 464), 0.0, OP.add, OP.min)
+    act(R("sig1", 0, C), (R("srow", 0, 512), xs1))
+    four("e", R("lq", 0, C), R("ls", 0, C), C)
+    for t in range(4):
+        mov("SVSV"[t], plane("tph", C, t), bank(2 + t, C), 0.5)
 
-    def make_p(lst, win, ww, wn, first, zt, qi, pt, qp, sp, gap1, gap2):
-        for t in range(4):
-            ev = plane("hp", HW, t, 225, 673, 2) if first else plane("ztmp", H, t)
-            if t == 0:
-                st = ev[3]
-                act(R(ev[0], ev[1], ev[1] + 128 * st, st), (plane(win, ww, t, 0, wn), sub(lst, 0, 8)))
-                cp(R(ev[0], ev[1] + 128 * st, ev[2], st), (plane(win, ww, t, 0, wn), sub(lst, 8, 14)))
-            else:
-                act(ev, (plane(win, ww, t, 0, wn), sub(lst, 0, 14)))
-            tt(word(zt, t, 0, H), (plane(win, ww, t, 0, wn), sub(lst, 14, 28)), ev, OP.add)
-        qz, sz = R("qa", H * qi, H * qi + H), R("sa", H * qi, H * qi + H)
-        quant(qz, sz, R(zt, 0, 4 * H))
-        four("w", qz, sz, H)
-        gap1()
-        if first:
-            for t in (0, 1):
-                act(plane("hp", HW, t, 226, 674, 2), (plane(win, ww, t), sub(lst, 14, 28)))
-        for t in range(4):
-            mov("SV"[t % 2], word(pt, t, 0, H), bank(2 + t, H), 0.03125)
-        quant(R(qp, 0, H), R(sp, 0, H), R(pt, 0, 4 * H))
-        mm(bank(6, H), qr, sr, R(qp, 0, H), R(sp, 0, H))
-        mm(bank(7, H), qr, sr, R(qp, 0, H), R(sp, 0, H))
-        gap2()
-        if first:
-            for t in (2, 3):
-                act(plane("hp", HW, t, 226, 674, 2), (plane(win, ww, t), sub(lst, 14, 28)))
+
+    def make_p(lst, win, ww, wn, first, zt, qi, pt, qp, sp):
+        def ev(t, lo, hi):
+            return plane("hp", HW, t, 225 + 2 * lo, 225 + 2 * hi, 2) if first else plane("ztmp", H, t, lo, hi)
+
+        def pick(t, half, lo, hi):
+            return (plane(win, ww, t, 0, wn), sub(lst, 14 * half + lo // 16, 14 * half + hi // 16))
+
+        cp(ev(3, 0, H), pick(3, 0, 0, H))
+        for j, (lo, hi, m0) in enumerate(RUNS):
+            for t in range(3):
+                act(ev(t, lo, hi), pick(t, 0, lo, hi))
+            for t in range(4):
+                tt(word(zt, t, lo, hi), pick(t, 1, lo, hi), ev(t, lo, hi), OP.add)
+            quant(R("qa", H * qi + m0, H * qi + hi), R("sa", H * qi + m0, H * qi + hi), R(zt, 4 * m0, 4 * hi))
+            four("w", R("qa", H * qi + m0, H * qi + hi), R("sa", H * qi + m0, H * qi + hi), hi - m0)
+            for t in range(4):
+                mov(COPIES[j][t], word(pt, t, lo, hi), bank(2 + t, hi - m0, lo - m0), 0.03125)
+            quant(R(qp, m0, hi), R(sp, m0, hi), R(pt, 4 * m0, 4 * hi))
+            for b in SCORES[j]:
+                mm(bank(b, hi - m0), qr, sr, R(qp, m0, hi), R(sp, m0, hi))
 
     def merge(row, hold, w, xo, sig, creset, grow, gw, places):
         m1 = 14 * w
-        ob, cb, c2 = of(28), sm(14), sm(14)
+        hh, ns = H // 2, 14 - NVM[places == H]
+        ob, off, o_v = of(28), of(14), of(14)
+        cb, c2, c3, lt, gt, dif, own, a = (sm(14) for _ in range(8))
         ends = R("f1s", w - 1, m1, w)
-        steps = {
-            "V0": lambda i: tt(R("f1", 0, m1), (R(hold, 0, H), xo), R(sig, 0, m1), OP.is_ge),
-            "S0": lambda: act(R("pdup", 0, C), (R(row, 0, H), xd)),
-            ("V", 0): lambda i: scan(R("f1s", 0, m1), R(creset, 0, m1), R("f1", 0, m1), 0.0, OP.mult, OP.add),
-            ("V", 1): lambda i: (ts(sub(ob, 0, 28, 2), ends, col(5), OP.max), ts(sub(ob, 1, 28, 2), ends, col(6), OP.max),
-                                 ts(cb, ends, 16.0, OP.mult, -1.0, OP.add)),
-            ("V", 2): lambda i: (tt(R("f2", 0, C), (R("srtw", 0, 32), ob), R("pdup", 0, C), OP.is_le),
-                                 tt(c2, cb, R("eup", 15, H, 16), OP.subtract)),
-            ("V", 3): lambda i: add("V", lambda q: q.transpose(T.f2t[:], T.f2[:]), [R("f2", 0, C)], [R("f2t", 0, C)]),
-            ("V", 4): lambda i: scan(R("f2s", 0, C), R("c32", 0, C), R("f2t", 0, C), 0.0, OP.mult, OP.add),
-            ("V", 5): lambda i: tt(i, c2, R("f2s", 31, C, 32), OP.add),
-        }
-        a, done = ranks(H, [(6, 7)], row, hold, NVM, steps, R(grow, 0, gw), "idr")
+
+        def held(k):
+            return R(hold, 16 * k + 15, 16 * k + 16)
+
+        def flags(k):
+            e = 16 * k + 16
+            ts(R("fl", H * k, H * k + e), R(row, 0, e), held(k), OP.is_le)
+            if e < H:
+                ts(R("fl", H * k + e, H * k + H), R(row, e, H), held(k), OP.is_lt)
+
+        def total(k):
+            scan(R("sc", hh * k, hh * k + hh), R("fl", H * k, H * k + hh), R("fl", H * k + hh, H * k + H), sub(c3, k, k + 1), OP.add, OP.add)
+
+        for j, (lo, hi, m0) in enumerate(RUNS):
+            b_v, b_s = (bank(b, hi - m0, lo - m0) for b in SCORES[j])
+            act(R(row, lo, hi), b_s)
+            tt(R("mm", lo, hi), b_v, R("mask", lo, hi), OP.mult)
+            scan(R(hold, lo, hi), R("nmask", lo, hi), R("mm", lo, hi), 0.0, OP.mult, OP.add)
+            act(R("pdup", 2 * lo, 2 * hi), (R(row, 0, hi), sub(xd, lo // 8, hi // 8)))
+        for j, (lo, hi, m0) in enumerate(RUNS):
+            k0, k1 = lo // 16, hi // 16
+            end = R("f1s", w * k0 + w - 1, w * k1, w)
+            tt(R("f1", w * k0, w * k1), (R(hold, 0, hi), sub(xo, w * k0 // 16, w * k1 // 16)), R(sig, w * k0, w * k1), OP.is_ge)
+            tt(R("eq", lo, hi), bank(SCORES[j][0], hi - m0, lo - m0), R(hold, lo, hi), OP.is_equal)
+            scan(R("f1s", w * k0, w * k1), R(creset, w * k0, w * k1), R("f1", w * k0, w * k1), 0.0, OP.mult, OP.add)
+            ts(sub(ob, 2 * k0, 2 * k1, 2), end, 16.0, OP.mult, col(5), OP.max)
+            ts(sub(ob, 2 * k0 + 1, 2 * k1, 2), end, 16.0, OP.mult, col(6), OP.max)
+            tt(R("f2", 2 * lo, 2 * hi), (R("shold", 16, 465), sub(ob, 2 * k0, 2 * k1)), R("pdup", 2 * lo, 2 * hi), OP.is_le)
+        scan(R("eup", 0, H), R("eq", 0, H), R("nmask", 0, H), 0.0, OP.add, OP.mult)
+        for k in range(ns):
+            act(R("sg", H * k, H * k + H), R(row, 0, H), AF.Sign, held(k), -1.0)
+        for k in range(ns):
+            lo = R("sg", H * k, H * k + 16 * k + 16)
+            act(lo, lo, AF.Relu, None, -1.0, sub(gt, k, k + 1))
+        for k in range(ns):
+            hi = R("sg", H * k + 16 * k + 16, H * k + H)
+            act(hi, hi, AF.Relu, None, None, sub(lt, k, k + 1))
+        vs = list(range(ns, 14))
+        turn(R("f2t", 0, C), R("f2", 0, C))
+        ts(cb, ends, 16.0, OP.mult, -1.0, OP.add)
+        flags(vs[0])
+        scan(R("f2s", 0, C), R("c32", 0, C), R("f2t", 0, C), 0.0, OP.mult, OP.add)
+        tt(c2, cb, R("eup", 15, H, 16), OP.subtract)
+        flags(vs[1])
+        tt(c3, c2, R("f2s", 31, C, 32), OP.add)
+        for k in vs[2:]:
+            flags(k)
+        tt(sub(dif, 0, ns), R("iot", 78, 78 + ns), sub(gt, 0, ns), OP.subtract)
+        for k in vs:
+            total(k)
+        tt(sub(own, 0, ns), sub(dif, 0, ns), sub(c3, 0, ns), OP.add)
+        sums = R("sc", hh * ns + hh - 1, hh * 14, hh)
+        cp(sub(o_v, 0, 14 - ns), sums)
+        tt(sub(a, 0, ns), sub(own, 0, ns), sub(lt, 0, ns), OP.add)
+        cp((R(grow, 0, gw), sub(o_v, 0, 14 - ns)), R("idr", 16 * ns, H))
+        cp(sub(off, 0, ns), sub(a, 0, ns))
+        cp(sub(a, ns, 14), sums)
+        cp((R(grow, 0, gw), sub(off, 0, ns)), R("idr", 0, 16 * ns))
         nk, st = places // 16, places // H
+        d1, d2, lst = sm(nk), sm(nk), of(nk)
         scan(R("cum", 0, places), R(grow, 0, places), R(grow, 0, places), 224.0, OP.add, OP.max)
         for j in range(st):
             diag(R("dgb", H * j, H * j + H), R(grow, j, places, st))
         for j in range(st):
             diag(R("dgc", H * j, H * j + H), R("cum", j, places, st))
-        d1, d2, lst = sm(nk), sm(nk), of(nk)
-        ts(d1, R("dgb", 15, places, 16), 2.0 ** 17, OP.mult)
+            if j == 0:
+                ts(d1, R("dgb", 15, places, 16), 2.0 ** 17, OP.mult)
         tt(d2, d1, R("dgc", 15, places, 16), OP.min)
         ts(lst, d2, col(3), OP.mult)
-        return a, lst, done
+        return a, lst
 
-    make_p(R("ll", 0, 28), "tph", C, C, True, "z1", 0, "p1", "qp1", "sp1",
-           lambda: mset(R("at2", 0, HW), 225.0), lambda: mset(R("g2", 0, 496), 1.0))
+    make_p(R("ll", 0, 28), "tph", C, C, True, "z1", 0, "p1", "qp1", "sp1")
     send("mp", {"q": ("qp1", 0), "s": ("sp1", 0)})
-    a1, l1, done = merge("row1", "hold1", 32, x1, "sig1", "c32", "g1", 672, C)
+    gfill(R("g2", 0, 496), 1)
+    gfill(R("at2", 0, HW), 225)
+    a1, l1 = merge("row1", "hold1", 32, x1, "sig1", "c32", "g1", 672, C)
     send("l1", {"l": ("of", l1[1])})
+    for t in range(4):
+        act(plane("hp", HW, t, 226, 674, 2), (plane("tph", C, t), R("ll", 14, 28)))
     four("e", R("lq", C, C + H), R("ls", C, C + H), H)
     for t in range(4):
         act(plane("hp", HW, t, 1, 225), bank(2 + t, H), AF.Copy, None, 0.5)
-    done()
     cp((R("at1", 0, HW), sub(l1, 0, 14)), R("jrow", 0, H))
     cp((R("at1", 0, HW), sub(l1, 14, 28)), R("jrow", 0, H))
     o_b1 = halved(a1, 14)
     send("k1", {"l": ("of", o_b1[1])})
     act(R("sig2", 0, H), (R("srow", 0, 512), xs2))
-    fill(R("ho", 0, 4 * OW, OW), 0.0)
-    for nm in ("v8", "d1", "d0"):
-        fill(R(nm, H, 4 * VW, VW), 0.0)
-    fill(R("mr", H, 3 * VW, VW), 225.0)
     act(R("c16", 0, H), R("tm", 0, H), AF.Sign)
     for t in range(4):
         for j in range(2):
-            mov("SV"[t % 2], plane("ho", OW, t, 225 + j, 449, 2), (plane("t8", C, t), sub(l0, 14 * j, 14 * j + 7)), 8.0)
+            mov("SSSV"[t], plane("ho", OW, t, 225 + j, 449, 2), (plane("t8", C, t), sub(l0, 14 * j, 14 * j + 7)), 8.0)
     act(R("ag1", 0, C), (R("at1", 0, HW), o_r))
+    o_x0 = halved(r0, 28)
+    o_x1 = to_offsets(R("ag1", 0, C), 1)
+    quant(R("qv", 0, 128), R("sv", 0, 128), R("vt", 0, 512))
 
-    x1o = []
-    make_p(R("ll", 32, 60), "hp", HW, 673, False, "z2", 1, "p2", "qp2", "sp2",
-           lambda: x1o.append(to_offsets(R("ag1", 0, C), 1)), lambda: None)
-    o_x1 = x1o[0]
+    make_p(R("ll", 32, 60), "hp", HW, 673, False, "z2", 1, "p2", "qp2", "sp2")
+    a2, l2 = merge("row2", "hold2", 16, x2, "sig2", "c16", "g2", 496, H)
     four("e", R("qp2", 0, H), R("sp2", 0, H), H)
-    a2, l2, done = merge("row2", "hold2", 16, x2, "sig2", "c16", "g2", 496, H)
     for t in range(4):
         act(plane("ho", OW, t, 1, 225), bank(2 + t, H))
-    for t in range(4):
-        mov("SV"[t % 2], word("e2", t, 0, H), (plane("ho", OW, t, 0, 449), l2))
-    qz, sz = R("qa", 2 * H, 3 * H), R("sa", 2 * H, 3 * H)
-    quant(qz, sz, R("e2", 0, 4 * H))
-    four("w", qz, sz, H)
-    done()
     o_b2 = of(14)
     ts(o_b2, a2, 224.0, OP.min)
     send("k2", {"l": ("of", o_b2[1])})
+    for nm in ("b2", "b1"):
+        fill(R(nm, 4 * H, 4 * BW), 0.0)
+
+    def products(w, j, q_, s_):
+        for b in range(4):
+            mm(bank(BANKS[j][b], size(q_)), R("q" + w, 128 * b, 128 * b + 128), R("s" + w, 128 * b, 128 * b + 128), q_, s_)
+
+    for j, (lo, hi, m0) in enumerate(BACK):
+        for t in range(4):
+            mov("SV"[t % 2], word("e2", t, lo, hi), (plane("ho", OW, t, 0, 449), sub(l2, lo // 16, hi // 16)))
+        q0 = (2 + j) * H
+        quant(R("qa", q0, q0 + hi - m0), R("sa", q0, q0 + hi - m0), R("e2", 4 * m0, 4 * hi))
+        products("w", j, R("qa", q0, q0 + hi - m0), R("sa", q0, q0 + hi - m0))
 
     def hand_back(k, bt, qb, sb, msg, vals, kv):
-        for t in range(4):
-            mov("SV"[t % 2], word(bt, t, 0, H), bank(2 + t, H), k)
-        quant(R(qb, 0, H), R(sb, 0, H), R(bt, 0, 4 * H))
+        for j, (lo, hi, m0) in enumerate(BACK):
+            for t in range(4):
+                mov("SV"[t % 2], word(bt, t, lo, hi), bank(BANKS[j][t], hi - m0, lo - m0), k)
+            end = max(hi, lo + 128)
+            quant(R(qb, lo, end), R(sb, lo, end), R(bt, 4 * lo, 4 * end))
+        aside(True)
         send(msg, {"q": (qb, 0), "s": (sb, 0)})
-        for t in range(4):
-            act(plane(vals, VW, t, 0, H), bank(2 + t, H), AF.Copy, None, kv)
+        for j, (lo, hi, m0) in enumerate(BACK):
+            for t in range(4):
+                act(plane(vals, VW, t, lo, hi), bank(BANKS[j][t], hi - m0, lo - m0), AF.Copy, None, kv)
 
     def landed(m):
         return R("ll", BASE[m], BASE[m] + 14)
@@ -607,9 +876,13 @@ def rank_program(g, core, T, topo):
     hand_back(0.03125, "b2", "qb2", "sb2", "m2", "v8", 2.0 ** -8)
     rid, pid = topo.addr(prv2, core)
     add("G", lambda q: q.remote_dma(T.ll[:, BASE["k3"]:BASE["k3"] + 14], ap(o_b2), T.sem.a_k3, T.sem.lsent, pid, rid, topo.mask(core, prv2)),
-        [o_b2], [], remote=True)
+        [o_b2], [], ISSUE, remote="k3")
     sent[0] += len(topo.engines(core, prv2))
     cp((R("at2", 0, HW), l2), R("jrow", 0, H))
+    aside(False)
+    for nm in ("v8", "d1", "d0"):
+        fill(R(nm, H, 4 * VW, VW), 0.0)
+    fill(R("mr", H, 3 * VW, VW), 225.0)
     act(R("ag2", 0, C), (R("at2", 0, HW), o_r))
     o_x2 = to_offsets(R("ag2", 0, C), 2)
     jw = R("jrow", 0, 225)
@@ -619,8 +892,10 @@ def rank_program(g, core, T, topo):
     for t in range(4):
         tt(plane("y2", C, t), (plane("v8", VW, t, 0, 225), o_x2), plane("t8", C, t), OP.add)
 
-    four("e", R("lq", C + H, C + 2 * H), R("ls", C + H, C + 2 * H), H)
+    for j, (lo, hi, m0) in enumerate(BACK):
+        products("e", j, R("lq", C + H + m0, C + H + hi), R("ls", C + H + m0, C + H + hi))
     hand_back(None, "b1", "qb1", "sb1", "m1", "d1", 0.25)
+    aside(False)
     o_y1 = to_offsets(R("ix", 0, C), 3)
     act(plane("mr", VW, 1, 0, H), (jw, landed("k3")))
     act(plane("mr", VW, 2, 0, H), (plane("mr", VW, 1, 0, 225), landed("k1")))
@@ -633,19 +908,28 @@ def rank_program(g, core, T, topo):
     ts(R("un", 2 * C, 3 * C), R("ix", C, 2 * C), 224.0, OP.max, -232.0, OP.add)
     scan(R("un", 4 * C, 5 * C), R("un", 3 * C, 4 * C), R("un", 2 * C, 3 * C), -64.0, OP.max, OP.add)
 
+    act(R("ucr", 0, C), R("un", 4 * C, 5 * C), AF.Identity, -13.0, -1.0)
+    dma("Y", T.uc[:], T.ucr[0:128:16, :], [R("ucr", 0, C)], [], 6.0)
+
     four("e", R("lq", C + 2 * H, C + 3 * H), R("ls", C + 2 * H, C + 3 * H), H)
     for t in range(4):
         act(plane("d0", VW, t, 0, H), bank(2 + t, H), AF.Copy, None, 0.5)
-    act(R("ucr", 0, C), R("un", 4 * C, 5 * C), AF.Identity, -13.0, -1.0)
-    dma("Y", T.uc[:], T.ucr[0:128:16, :], [R("ucr", 0, C)], [])
-    for j, (lo, hi) in enumerate(((0, 320), (320, C))):
-        for t in range(4):
+
+    def last(j, ts_):
+        lo, hi = CHUNKS[j]
+        for t in ts_:
             tt(word("xf", t, lo, hi), (plane("d0", VW, t, 0, 225), sub(o_y0, lo // 16, hi // 16)), plane("y1", C, t, lo, hi), OP.add)
+
+    last(0, (0,))
+    for j, (lo, hi) in enumerate(CHUNKS):
+        last(j, (1, 2, 3))
+        if j + 1 < len(CHUNKS):
+            last(j + 1, (0,))
         quant(R("qo", lo, hi), R("so", lo, hi), R("xf", 4 * lo, 4 * hi))
-        mm(bank(j, hi - lo), R("qv", 0, 128), R("sv", 0, 128), R("qo", lo, hi), R("so", lo, hi))
-        dma("Y", T.oc[:, 4 * lo:4 * hi], T.qo[:, lo:hi].bitcast(dt.uint8), [R("qo", lo, hi)], [])
-        act(R("yo", lo, hi), bank(j, hi - lo))
-        dma("S", T.y[:, lo:hi], T.yo[:, lo:hi], [R("yo", lo, hi)], [])
+        mm(bank((0, 1, 6)[j], hi - lo), R("qv", 0, 128), R("sv", 0, 128), R("qo", lo, hi), R("so", lo, hi))
+        dma("Y", T.oc[:, 4 * lo:4 * hi], T.qo[:, lo:hi].bitcast(dt.uint8), [R("qo", lo, hi)], [], 1.5 + OUT * (C - lo))
+        act(R("yo", lo, hi), bank((0, 1, 6)[j], hi - lo))
+        dma("S", T.y[:, lo:hi], T.yo[:, lo:hi], [R("yo", lo, hi)], [], 1.5 + OUT * (C - lo))
     for k in range(4):
-        dma("Y", T.osc[4 * k:4 * k + 4, :], T.so[32 * k:32 * k + 4, :], [R("so", 0, C)], [])
+        dma("Y", T.osc[4 * k:4 * k + 4, :], T.so[32 * k:32 * k + 4, :], [R("so", 0, C)], [], 1.6)
     emit()

from concourse.bass import DstId, RemoteDMATransfer
from concourse.mybir import dt, AluOpType, ActivationFunctionType

OP = AluOpType
AF = ActivationFunctionType
C, H = 448, 224
HW = 688
OW = 464
VW = 240
BIG = 1.0e29
SH = 2.0 ** -20
DROP = -(2.0 ** 30)
NVA = 8
EARLY_V, EARLY_S, MID_V, MID_S = 2, 4, 2, 3
CHUNKS = ((0, 256), (256, 448))
RUNS = ((0, 128, 0), (128, H, 96))
SCORES, COPIES = ((6, 7), (0, 1)), ("SVSV", "SVSV")
BACK, BANKS, BW = ((0, 192, 0), (192, H, 96)), ((2, 3, 4, 5), (0, 1, 6, 7)), 320
NVM = (5, 5)
CYCLE, CALL, SETTLE, ISSUE, GATHER, SCATTER = 0.00088, 0.05, 0.18, 0.4, 1.56, 4.5
ROUNDS, HASTE, OUT, PLAN = 3, 1.0, 0.003, {}
PATIENCE = (0.05,)
WAY = {"ma": 16.0, "mb": 16.0, "l0": 3.0, "mp": 8.0, "l1": 3.0, "k1": 6.0, "k2": 5.5, "k3": 5.0, "m2": 4.3, "m1": 4.3}
F32, BF, U16, I32, FP4, U8, F16 = "float32", "bfloat16", "uint16", "int32", "float8_e4m3fn_x4", "uint8", "float16"


def _sb(n, d):
    return ("sbuf", [128, n], d)


SCRATCH = {
    "ps": ("psum", [128, 4096], F32),
    "xt": _sb(4 * C, BF), "ut": _sb(512, BF), "vt": _sb(512, BF),
    "qx": _sb(C, FP4), "sx": _sb(C, U8), "qu": _sb(128, FP4), "su": _sb(128, U8), "qr": _sb(128, FP4), "sr": _sb(128, U8),
    "qv": _sb(128, FP4), "sv": _sb(128, U8), "qw": _sb(512, FP4), "sw": _sb(512, U8),
    "et": _sb(2048, BF), "qe": _sb(512, FP4), "se": _sb(512, U8), "ones": _sb(C, BF), "idn": _sb(128, BF),
    "pc": _sb(1, I32), "ci": _sb(2, I32), "cf": _sb(16, F32), "tm": _sb(464, BF), "jrow": _sb(C, F32),
    "mask": _sb(464, BF), "nmask": _sb(C, BF), "cdg": _sb(H, BF), "cd1": _sb(32, BF), "cd2": _sb(32, BF),
    "c32": _sb(C, BF), "c16": _sb(H, BF), "idr": _sb(H, BF),
    "iot": _sb(128, F32), "uoff": _sb(8, U16), "coff": _sb(144, U16),
    "row0": _sb(C, F32), "row1": _sb(H, F32), "row2": _sb(H, F32), "mm": _sb(C, F32),
    "hold0": _sb(C, F32), "hold1": _sb(H, F32), "hold2": _sb(H, F32), "eq": _sb(C, BF), "eup": _sb(C, BF),
    "fl": _sb(20 * C, BF), "sc": _sb(20 * H, F16), "sg": _sb(14 * C, BF),
    "sm": _sb(640, F32), "of": _sb(448, U16), "si": _sb(192, I32),
    "g0": _sb(C, F32), "g1": _sb(672, BF), "g2": _sb(496, BF), "dg": _sb(C, F32), "dgb": _sb(5 * C, BF),
    "cum": _sb(C, F16), "dgc": _sb(C, F16),
    "xv": _sb(8 * C, BF), "xs": _sb(8 * 336, BF), "cs": _sb(8 * H + 16, BF), "cg": _sb(C, BF), "ct": _sb(C, BF), "cu": _sb(C, BF),
    "cbig": _sb(464, BF),
    "srow": _sb(512, F32), "shold": _sb(480, F32), "sig1": _sb(C, F32), "sig2": _sb(H, F32),
    "pdup": _sb(C, F32), "f1": _sb(C, BF), "f1s": _sb(C, BF), "f2": _sb(C, BF), "f2t": _sb(C, BF), "f2s": _sb(C, BF),
    "at1": _sb(HW, BF), "at2": _sb(HW, BF), "ag1": _sb(C, BF), "ag2": _sb(C, BF),
    "tph": _sb(4 * C, BF), "t8": _sb(4 * C, BF), "hp": _sb(4 * HW, BF), "ho": _sb(4 * OW, BF), "ztmp": _sb(4 * H, BF),
    "z1": _sb(4 * H, BF), "z2": _sb(4 * H, BF), "p1": _sb(4 * H, BF), "p2": _sb(4 * H, BF), "e2": _sb(4 * H, BF),
    "b2": _sb(4 * BW, BF), "b1": _sb(4 * BW, BF), "xf": _sb(4 * C, BF), "y2": _sb(4 * C, BF), "y1": _sb(4 * C, BF),
    "v8": _sb(4 * VW, BF), "d1": _sb(4 * VW, BF), "d0": _sb(4 * VW, BF),
    "qa": _sb(4 * H, FP4), "sa": _sb(4 * H, U8), "qp1": _sb(H, FP4), "sp1": _sb(H, U8), "qp2": _sb(H, FP4), "sp2": _sb(H, U8),
    "qb2": _sb(BW, FP4), "sb2": _sb(BW, U8), "qb1": _sb(BW, FP4), "sb1": _sb(BW, U8), "qo": _sb(C, FP4), "so": _sb(C, U8),
    "rq": _sb(C + 3 * H, FP4), "rs": _sb(C + 3 * H, U8), "lq": _sb(C + 3 * H, FP4), "ls": _sb(C + 3 * H, U8),
    "rl": _sb(112, U16), "ll": _sb(112, U16),
    "mr": _sb(3 * VW, BF), "ix": _sb(2 * C, BF), "un": _sb(5 * C, BF), "ucr": _sb(C, F32), "yo": _sb(C, F32),
}
MSGS = ["ma", "mb", "l0", "mp", "l1", "k1", "k2", "m2", "m1"]
SEMAPHORES = (["cV", "cS", "cT", "cG", "lsent", "a_k3"] + ["r_" + m for m in MSGS] + ["a_" + m for m in MSGS]
              + ["d%d" % i for i in range(24)])
BASE = {"ma": 0, "mb": H, "mp": C, "m2": C + H, "m1": C + 2 * H, "l0": 0, "l1": 32, "k1": 64, "k2": 80, "k3": 96}
FORWARD = ("ma", "mb", "l0", "mp", "l1")


def R(name, lo, hi, step=1):
    return (name, lo, hi, step)


def bank(b, n, lo=0):
    return ("ps", 512 * b + lo, 512 * b + n, 1)


def pieces(msg):
    if msg == "ma":
        return [[(i, "q", 56 * i, 56 * i + 56, "r_ma") for i in range(4)]]
    if msg == "mb":
        return [[(1, "q", 0, 112, "r_mb"), (3, "q", 112, H, "r_mb"), (2, "s", -H, H, "r_mb")]]
    if msg in ("m2", "m1"):
        return [[(0, "q", 0, 84, "r_" + msg), (2, "q", 84, 168, "r_" + msg)], [(1, "q", 168, H, "r_" + msg), (3, "s", 0, H, "r_" + msg)]]
    if msg == "mp":
        return [[(0, "q", 0, 112, "r_" + msg), (2, "q", 112, H, "r_" + msg)], [(1, "s", 0, H, "r_" + msg)]]
    if msg in ("l0", "l1"):
        return [[(0, "l", 0, 28, "r_" + msg)]]
    return [[(3, "l", 0, 14, "r_" + msg)]]


def share(engines, call):
    per = 1
    while 2 * per * len(call) <= len(engines):
        per *= 2
    return per


def relays_of(rank_core, far, topo):
    cs = [c for c in topo.cores_of(rank_core) if c != rank_core and topo.may_write(c, far)]
    near = [c for c in cs if topo.die(c) == topo.die(rank_core)]
    return near + [c for c in cs if c not in near]


def side(T, kind, who, lo, hi):
    ap = T[who + kind][:, lo:hi]
    return ap.bitcast(dt.uint8) if kind == "q" else ap


def mask_of(engines):
    m = 0
    for e in engines:
        m |= 1 << e
    return m


def relay_program(g, core, T, topo):
    owner = [c for c in topo.cores_of(core) if T.rank_of(c) is not None]
    if not owner:
        return
    rank = T.rank_of(owner[0])
    n = len(T.cores)
    nxt, prv = T.cores[(rank + 1) % n], T.cores[(rank - 1) % n]
    rel = relays_of(owner[0], nxt, topo)
    if core not in rel:
        return
    me = rel.index(core)
    sent = 0
    for msg in MSGS:
        dst = nxt if msg in FORWARD else prv
        for call in pieces(msg):
            for (i, kind, lo, hi, sem) in call:
                if i != me:
                    continue
                g.wait_ge(T.sem[sem], share(topo.engines(owner[0], core), call))
                rid, pid = topo.addr(dst, core)
                b = BASE[msg]
                g.remote_dma(side(T, kind, "l", b + lo, b + hi), side(T, kind, "r", b + lo, b + hi), T.sem["a_" + msg], T.sem.lsent,
                             pid, rid, topo.mask(core, dst))
                sent += len(topo.engines(core, dst))
    g.wait_ge(T.sem.lsent, sent)


def make_builder(g, T):
    ops, acc, sent, head, gate = [], {}, [0], [], [None]
    Q = {"V": g.vector, "S": g.scalar, "T": g.tensor, "G": g, "Y": g.sync}
    ndma = [0]

    def cols(r):
        if r[0] == "ps":
            return {r[1] // 512}
        return set(range(r[1], r[2], r[3]))

    def add(q, fn, reads, writes, busy, dma=0.0, remote=None):
        i = len(ops)
        deps = set()
        for r, w in [(r, False) for r in reads] + [(r, True) for r in writes]:
            cs = cols(r)
            lst = acc.setdefault(r[0], [])
            for (ocs, ow, oi, oq) in lst:
                if oi != i and (w or ow or (r[0] == "ps" and oq != q)) and not cs.isdisjoint(ocs):
                    deps.add(oi)
            lst.append((cs, w, i, q))
        tok = None
        if dma:
            tok = ("d%d" % ndma[0], 16)
            ndma[0] += 1
        ops.append({"q": q, "fn": fn, "deps": deps, "tok": tok, "need": bool(dma), "plain": not (dma or remote), "busy": busy,
                    "done": dma or busy + SETTLE, "msg": remote, "behind": gate[0]})
        return i

    def aside(on):
        gate[0] = len(ops) - 1 if on else None

    def arrival(msg, val, writes, way):
        i = add(None, None, [], writes, 0.0, remote=msg)
        ops[i]["tok"] = ("a_" + msg, val)
        ops[i]["done"] = way

    def mark():
        head.append(len(ops))

    def arrange():
        before = [set(o["deps"]) for o in ops]
        lead = [{} for o in ops]
        prev = {}
        for i, o in enumerate(ops):
            if o["q"] is None:
                lead[i] = {j: 0.0 for j, p in enumerate(ops) if p["q"] == "G" and p["msg"] == o["msg"]}
            elif not o["plain"] or o["q"] == "G":
                if o["q"] in prev:
                    lead[i] = {prev[o["q"]]: ops[prev[o["q"]]]["busy"]}
                prev[o["q"]] = i
            if o["behind"] is not None and o["q"] == "V":
                lead[i].setdefault(o["behind"], 0.0)
        edge = [{**lead[i], **{d: ops[d]["done"] for d in before[i]}} for i in range(len(ops))]
        back = [{} for o in ops]
        for i, e in enumerate(edge):
            for d, w in e.items():
                back[d][i] = w * (HASTE if ops[d]["q"] is None else 1.0) - ops[d]["busy"] + ops[i]["busy"]

        def fit(order, edges, first):
            at, taken = {}, {q: [] for q in Q}
            for i in order:
                t = max([first(i)] + [at[d] + w + 1e-6 for d, w in edges[i].items()])
                q, busy = ops[i]["q"], ops[i]["busy"]
                if q is not None:
                    for (a, b) in taken[q]:
                        if t + busy <= a:
                            break
                        t = max(t, b)
                    taken[q].append((t, t + busy))
                    taken[q].sort()
                at[i] = t
            return at

        def step(edges, follow, first, rank_, patience):
            at, free, left = {}, {q: 0.0 for q in list(Q) + [None]}, [len(e) for e in edges]
            ready = {i: first(i) for i in range(len(ops)) if not left[i]}
            while ready:
                soon = min(ready, key=lambda i: max(ready[i], free[ops[i]["q"]]))
                q = ops[soon]["q"]
                t0 = max(ready[soon], free[q])
                i = min((j for j in ready if ops[j]["q"] == q and ready[j] <= t0 + patience), key=rank_)
                at[i] = max(ready.pop(i), free[q])
                if q is not None:
                    free[q] = at[i] + ops[i]["busy"]
                for j in follow[i]:
                    left[j] -= 1
                    if not left[j]:
                        ready[j] = max([first(j)] + [at[d] + w + 1e-6 for d, w in edges[j].items()])
            return at

        def urgency(late):
            return lambda i: (0, i) if head[0] <= i < head[1] else (1, -late[i] - ops[i]["busy"])

        def tail(i):
            return ops[i]["done"] - ops[i]["busy"]

        best = PLAN.get(len(ops))
        for patience in () if best else PATIENCE:
            order = sorted(range(len(ops)), key=lambda i: max(lead[i]) + 0.5 if ops[i]["q"] is None else i)
            at = fit(order, edge, lambda i: 0.0)
            for _ in range(ROUNDS):
                if patience is None:
                    late = fit(sorted(at, key=lambda i: -at[i]), back, tail)
                    at = fit(sorted(late, key=urgency(late)), edge, lambda i: 0.0)
                else:
                    late = step(back, edge, tail, lambda i: -at[i], patience)
                    at = step(edge, back, lambda i: 0.0, urgency(late), patience)
                end = max(at[i] + ops[i]["done"] for i in at)
                if best is None or end < best[0]:
                    best = (end, at, patience)
        PLAN[len(ops)] = best
        for i, t in best[1].items():
            ops[i]["at"] = t
        new = sorted(range(len(ops)), key=lambda i: ops[i]["at"])
        place = {i: p for p, i in enumerate(new)}
        ops[:] = [ops[i] for i in new]
        for o in ops:
            o["deps"] = {place[d] for d in o["deps"]}

    def emit():
        arrange()
        for i, o in enumerate(ops):
            last = {}
            for d in o["deps"]:
                if ops[d]["tok"] is None:
                    last[ops[d]["q"]] = max(last.get(ops[d]["q"], -1), d)
            o["deps"] = [d for d in o["deps"] if ops[d]["tok"] is not None] + list(last.values())
        seen = {q: {} for q in Q}
        hist = {q: [] for q in Q}
        for i, o in enumerate(ops):
            if o["q"] is None:
                o["clock"] = {("t", i): 1}
                continue
            k = seen[o["q"]]
            keep = []
            for d in sorted(o["deps"], reverse=True):
                key, val = (("t", d), 1) if ops[d]["tok"] is not None else (ops[d]["q"], d)
                if k.get(key, -1) >= val:
                    continue
                if key == o["q"]:
                    d = max([d] + [j for j in hist[key][-12:] if ops[j]["at"] + ops[j]["done"] + 2 * SETTLE <= o["at"]])
                keep.append(d)
                ops[d]["need"] = True
                for kk, vv in ops[d]["clock"].items():
                    if k.get(kk, -1) < vv:
                        k[kk] = vv
            o["deps"] = keep
            o["clock"] = dict(k)
            if o["tok"] is not None:
                o["clock"][("t", i)] = 1
            else:
                o["clock"][o["q"]] = i
            if o["plain"]:
                hist[o["q"]].append(i)
        count = {q: 0 for q in Q}
        for o in ops:
            if o["q"] is not None and o["tok"] is None and o["need"]:
                count[o["q"]] += 1
                o["tok"] = ("c" + o["q"], count[o["q"]])
                o["inc"] = 1
        final = {}
        for o in ops:
            if o["tok"] is not None:
                final[o["tok"][0]] = o["tok"][1]
            if o["q"] is None:
                continue
            for d in o["deps"]:
                Q[o["q"]].wait_ge(T.sem[ops[d]["tok"][0]], ops[d]["tok"][1])
            ins = o["fn"](Q[o["q"]])
            if o["need"]:
                ins.then_inc(T.sem[o["tok"][0]], o.get("inc", 16))
        final["lsent"] = sent[0]
        for s, v in final.items():
            g.wait_ge(T.sem[s], v)

    return add, arrival, mark, aside, emit, sent


def rank_program(g, core, T, topo):
    rank = T.rank_of(core)
    if rank is None:
        relay_program(g, core, T, topo)
        return
    n = len(T.cores)
    nxt, prv2 = T.cores[(rank + 1) % n], T.cores[(rank - 2) % n]
    rel = relays_of(core, nxt, topo)
    add, arrival, mark, aside, emit, sent = make_builder(g, T)

    def ap(r):
        if len(r) == 2:
            return ap(r[0]).indirect(ap(r[1]))
        return T[r[0]][:, r[1]:r[2]:r[3]] if r[3] != 1 else T[r[0]][:, r[1]:r[2]]

    def rd(*rs):
        out = []
        for r in rs:
            if isinstance(r, tuple):
                out += list(r) if len(r) == 2 else [r]
        return out

    def val(s):
        return ap(s) if isinstance(s, tuple) else s

    def size(r):
        return 16 * size(r[1]) if len(r) == 2 else len(range(r[1], r[2], r[3]))

    def span(out, *ins, slow=None):
        if len(out) == 2:
            return CALL + size(out) * SCATTER * CYCLE
        if len(ins[0]) == 2:
            return CALL + size(out) * GATHER * CYCLE
        narrow = all(SCRATCH[r[0]][2] in (BF, F16, U16) for r in (out,) + ins)
        return CALL / 2 + max(64, size(out) * (slow or (0.5 if narrow else 1.0))) * CYCLE

    def ts(out, a, s1, op0, s2=None, op1=None):
        if op1 is None:
            add("V", lambda q: q.tensor_scalar(ap(out), ap(a), val(s1), None, op0), rd(a, s1), [out], span(out, a))
        else:
            add("V", lambda q: q.tensor_scalar(ap(out), ap(a), val(s1), val(s2), op0, op1), rd(a, s1, s2), [out], span(out, a))

    def tt(out, a, b, op):
        add("V", lambda q: q.tensor_tensor(ap(out), ap(a), ap(b), op), rd(a, b), [out], span(out, a, b, slow=1.0 if a[0] == "ps" else 2.0))

    def cp(out, a):
        if len(out) == 2:
            add("V", lambda q: q.tensor_copy(ap(out), ap(a)), rd(a, out[1]), [out[0]], span(out, a))
        else:
            add("V", lambda q: q.tensor_copy(ap(out), ap(a)), rd(a), [out], span(out, a))

    def scan(out, a, b, init, op0, op1):
        add("V", lambda q: q.tensor_tensor_scan(ap(out), ap(a), ap(b), val(init), op0, op1), rd(a, b, init), [out], span(out, a, b))

    def turn(out, a):
        add("V", lambda q: q.transpose(ap(out), ap(a)), [a], [out], span(out, a))

    def mset(out, v):
        add("V", lambda q: q.memset(ap(out), v), [], [out], span(out, out))

    def act(out, a, f=AF.Copy, bias=None, scale=None, accum=None):
        kw = {}
        if bias is not None:
            kw["bias"] = val(bias)
        if scale is not None:
            kw["scale"] = val(scale)
        if accum is not None:
            kw["accum_out"] = ap(accum)
        add("S", lambda q: q.activation(ap(out), ap(a), f, **kw), rd(a, bias, scale), [out] + rd(accum),
            span(out, a, slow=1.0) + CALL / 2 + (0.02 if accum else 0.0))

    def fill(out, v):
        m = len(range(out[1], out[2], out[3]))
        act(out, R("ones", 0, m), AF.Identity, v, 0.0)

    def mov(e, out, a, k=None):
        if e == "S":
            act(out, a, AF.Copy, scale=k)
        elif k is None:
            cp(out, a)
        else:
            ts(out, a, k, OP.mult)

    def quant(q_, s_, a):
        add("V", lambda q: q.quantize_mx(ap(q_), ap(s_), ap(a)), [a], [q_, s_], 0.012 + 0.00022 * size(a))

    def mm(out, lq, ls, rq, rs):
        add("T", lambda q: q.matmul_mx(ap(out), ap(lq), ap(ls), ap(rq), ap(rs), True, True), [lq, ls, rq, rs], [out],
            (size(rq) + 16) * 0.0006)

    def four(w, q_, s_, m, b0=2):
        for b in range(4):
            mm(bank(b0 + b, m), R("q" + w, 128 * b, 128 * b + 128), R("s" + w, 128 * b, 128 * b + 128), q_, s_)

    def iota(out, pat, base, cm=0):
        kw = {} if out[0] == "pc" else {"allow_small_or_imprecise_dtypes": True}
        add("G", lambda q: q.iota(ap(out), pat, base, cm, **kw), [], [out], 0.13 + 2.4 * size(out) * CYCLE)

    def dma(e, out, in_, reads, writes, way):
        add(e, lambda q: q.dma_start(out, in_), reads, writes, CALL, dma=way)

    def send(msg, src):
        for call in pieces(msg):
            eng = topo.engines(core, rel[0])
            per = share(eng, call)
            trs, reads = [], []
            for j, (i, kind, lo, hi, sem) in enumerate(call):
                name, b0 = src[kind]
                s = T[name][:, b0 + lo:b0 + hi]
                rid, pid = topo.addr(rel[i], core)
                trs.append((s.bitcast(dt.uint8) if kind == "q" else s, side(T, kind, "r", BASE[msg] + lo, BASE[msg] + hi),
                            T.sem[sem], pid, rid, mask_of(eng[j * per:j * per + per])))
                reads.append(R(name, b0 + lo, b0 + hi))
            sent[0] += per * len(call)
            if len(trs) == 1:
                t = trs[0]
                add("G", lambda q, t=t: q.remote_dma(t[1], t[0], t[2], T.sem.lsent, t[3], t[4], t[5]), reads, [], ISSUE, remote=msg)
            else:
                add("G", lambda q, trs=trs: q.remote_dma_fused(
                    [RemoteDMATransfer(dst_ids=[DstId(rid=t[4], pnc=t[3])], dma_engine_mask=t[5], remote_sem=t[2], src=t[0], dst=t[1])
                     for t in trs], local_sem=T.sem.lsent), reads, [], ISSUE, remote=msg)

    far = len(topo.engines(rel[0], nxt))
    for msg in MSGS:
        ps_ = [p for call in pieces(msg) for p in call]
        arrival(msg, far * len(ps_), [R("l" + k, BASE[msg] + lo, BASE[msg] + hi) for (i, k, lo, hi, s) in ps_],
                WAY[msg])
    arrival("k3", len(topo.engines(T.cores[(rank + 2) % n], core)), [R("ll", BASE["k3"], BASE["k3"] + 14)], WAY["k3"])

    def col(j):
        return R("cf", j, j + 1)

    smp, ofp, sip = [0], [0], [0]

    def sm(w):
        smp[0] += w
        return R("sm", smp[0] - w, smp[0])

    def of(w):
        ofp[0] += w
        return R("of", ofp[0] - w, ofp[0])

    def sub(r, lo, hi, step=1):
        return R(r[0], r[1] + lo, r[1] + hi, step)

    def plane(name, w, t, lo=0, hi=None, step=1):
        return R(name, w * t + lo, w * t + (w if hi is None else hi), step)

    def word(name, t, lo, hi):
        return R(name, 4 * lo + t, 4 * hi, 4)

    mark()
    dma("S", T.ut[:], T.u[:], [], [R("ut", 0, 512)], 1.9)
    for j in range(2):
        dma("Y", T.xt[:, 4 * H * j:4 * H * j + 4 * H], T.x[:, 4 * H * j:4 * H * j + 4 * H], [], [R("xt", 4 * H * j, 4 * H * j + 4 * H)],
            2.8 + 0.9 * j)
    iota(R("pc", 0, 1), [[0, 1]], 0, 1)
    mset(R("ones", 0, C), 1.0)
    mset(R("et", 0, 2048), 0.0)
    fill(R("c32", 0, C), 1.0)
    for nm in ("xv", "xs"):
        fill(R(nm, 7, 8 * H, 8), DROP)
    fill(R("cs", 0, 8), 0.0)
    fill(R("srow", C, 512), BIG)
    fill(R("c32", 0, C, 32), 0.0)
    for nm, w in (("hp", HW), ("ho", OW)):
        fill(R(nm, 0, 4 * w, w), 0.0)
    iota(R("iot", 0, 8), [[16, 8]], 0)
    iota(R("tm", 0, 464), [[0, 29], [1, 16]], 0)
    add("G", lambda q: q.affine_select(T.idn[:], T.ones[:, 0:128], [[-1, 128]], OP.is_equal, 0.0, 0, 1), [R("ones", 0, 128)], [R("idn", 0, 128)], 0.45)
    iota(R("iot", 78, 106), [[16, 28]], 16)
    iota(R("iot", 106, 120), [[128, 14]], 14)
    iota(R("iot", 8, 36), [[16, 14], [0, 2]], 15)
    iota(R("iot", 36, 50), [[16, 14]], 15)
    iota(R("iot", 50, 78), [[0, 14], [256, 2]], 15)
    iota(R("jrow", 0, C), [[1, C]], 1)
    ts(R("ci", 0, 1), R("pc", 0, 1), 15, OP.bitwise_and)
    ts(R("ci", 1, 2), R("pc", 0, 1), 4, OP.logical_shift_right, 1, OP.bitwise_and)
    cp(R("uoff", 0, 8), R("iot", 0, 8))
    cp(R("cf", 0, 2), R("ci", 0, 2))
    ts(R("mask", 0, 464), R("tm", 0, 464), col(0), OP.is_equal)
    ts(R("nmask", 0, C), R("tm", 0, C), col(0), OP.not_equal)
    quant(R("qu", 0, 128), R("su", 0, 128), R("ut", 0, 512))
    add("V", lambda q: q.tensor_copy(T.qr[:, 0:128].bitcast(dt.uint32), T.qu[:, 0:128].bitcast(dt.uint32).indirect(T.uoff[:, 0:8])),
        [R("qu", 0, 128), R("uoff", 0, 8)], [R("qr", 0, 128)], 0.23)
    add("S", lambda q: q.activation(T.sr[:, 0:128], T.su[:, 0:128].indirect(T.uoff[:, 0:8]), AF.Copy),
        [R("su", 0, 128), R("uoff", 0, 8)], [R("sr", 0, 128)], 0.25)
    x1, x2, xd, xs1, xs2 = R("coff", 0, 28), R("coff", 28, 42), R("coff", 42, 70), R("coff", 70, 98), R("coff", 98, 112)
    xc = R("coff", 112, 140)
    qr, sr = R("qr", 0, 128), R("sr", 0, 128)

    def constants():
        for b in range(4):
            act(R("et", 512 * b + b, 512 * b + 512, 4), R("idn", 0, 128))
        act(col(4), col(0), AF.Copy, None, 16.0)
        act(col(5), col(1), AF.Copy, None, 448.0)
        act(col(6), col(1), AF.Identity, 448.0, -448.0)
        act(col(7), col(0), AF.Copy, None, 8.0)
        for j in range(2):
            quant(R("qe", 256 * j, 256 * j + 256), R("se", 256 * j, 256 * j + 256), R("et", 1024 * j, 1024 * j + 1024))
        act(R("cd1", 0, 32), R("mask", 15, 47), AF.Identity, 1.0, -(1.0 - SH))
        act(R("cd2", 0, 32), R("mask", 16, 48), AF.Copy, None, 2.0 ** 60)
        act(col(8), col(1), AF.Identity, col(7), -4096.0)
        act(col(9), col(6), AF.Identity, col(7), -16.0)
        act(col(3), R("mask", 15, 16), AF.Identity, 1.0 / SH, 1.0 - 1.0 / SH)
        tt(R("cdg", 0, 32), R("cd1", 0, 32), R("cd2", 0, 32), OP.max)
        for lo, hi in ((32, 64), (64, 128), (128, H)):
            act(R("cdg", lo, hi), R("cdg", 0, hi - lo))
        ts(sub(xc, 0, 28, 2), R("iot", 106, 120), col(8), OP.add)
        ts(sub(xc, 1, 28, 2), R("iot", 106, 120), col(9), OP.add)

    def gfill(out, v):
        iota(out, [[0, len(range(out[1], out[2], out[3]))]], v)

    def first_ranks():
        hk, hh = 14, H // 2
        nsa = hk - NVA
        a_s, a_v, b_s, b_v = list(range(nsa)), list(range(nsa, hk)), list(range(hk, hk + 7)), list(range(hk + 7, 2 * hk))
        lt, gt, init, base, dif, pre, out = (sm(28) for _ in range(7))
        o_a, o_bs, o_bv = of(hk), of(8), of(8)

        def held(k):
            return R("hold0", 16 * k + 15, 16 * k + 16)

        def scores(j):
            lo, hi = H * j, H * j + H
            quant(R("qx", lo, hi), R("sx", lo, hi), R("xt", 4 * lo, 4 * hi))
            for b in (6 * j, 6 * j + 1):
                mm(bank(b, H), qr, sr, R("qx", lo, hi), R("sx", lo, hi))
            send(("ma", "mb")[j], {"q": ("qx", lo), "s": ("sx", lo)})

        def row(j):
            act(R("row0", H * j, H * j + H), bank(6 * j + 1, H))

        def masked(j):
            tt(R("mm", H * j, H * j + H), bank(6 * j, H), R("mask", 0, H), OP.mult)

        def hold(j):
            scan(R("hold0", H * j, H * j + H), R("nmask", 0, H), R("mm", H * j, H * j + H), 0.0, OP.mult, OP.add)

        def equal(j):
            tt(R("eq", H * j, H * j + H), bank(6 * j, H), R("hold0", H * j, H * j + H), OP.is_equal)

        def behind(j):
            scan(R("eup", H * j, H * j + H), R("eq", H * j, H * j + H), R("nmask", 0, H), 0.0, OP.add, OP.mult)

        def start(j):
            ts(sub(init, hk * j, hk * j + hk), R("eup", H * j + 15, H * j + H, 16), -1.0, OP.mult, (111.0, -1.0)[j], OP.add)

        def v_flags(k):
            e, m = 16 * k + 16, H if k < hk else C
            ts(flag(k, 0, e), R("row0", 0, e), held(k), OP.is_le)
            if e < m:
                ts(flag(k, e, m), R("row0", e, m), held(k), OP.is_lt)

        def flag(k, lo, hi):
            return R("fl", H * k + lo, H * k + hi) if k < hk else R("xv", 8 * lo + k - b_v[0], 8 * hi, 8)

        def v_sum(k):
            h, s0 = (hh, hh * k) if k < hk else (H, H * (k - hk))
            scan(R("sc", s0, s0 + h), flag(k, 0, h), flag(k, h, 2 * h), sub(init, k, k + 1), OP.add, OP.add)

        def sg(k, lo, hi):
            b0 = H * k if k < hk else H * nsa + C * (k - hk)
            return R("sg", b0 + lo, b0 + hi)

        def s_sign(k):
            m = H if k < hk else 16 * k + 16
            act(sg(k, 0, m), R("row0", 0, m), AF.Sign, held(k), -1.0)

        def s_rest(k):
            act(sg(k, 16 * k + 16, C), R("row0", 16 * k + 16, C), AF.Sign, held(k), -1.0)

        def s_above(k):
            e = 16 * k + 16
            act(sg(k, 0, e) if k < hk else R("xs", k - hk, 8 * e, 8), sg(k, 0, e), AF.Relu, None, -1.0, sub(gt, k, k + 1))

        def s_below(k):
            e, m = 16 * k + 16, H if k < hk else C
            act(sg(k, e, m), sg(k, e, m), AF.Relu, None, None, sub(lt, k, k + 1))

        def each(f, ks):
            for k in ks:
                f(k)

        scores(0)
        row(0)
        masked(0)
        hold(0)
        each(s_sign, a_s[:EARLY_S])
        constants()
        mark()
        equal(0)
        v_flags(a_v[0])
        scores(1)
        row(1)
        each(s_sign, a_s[EARLY_S:])
        behind(0)
        each(v_flags, a_v[1:EARLY_V])
        masked(1)
        start(0)
        hold(1)
        each(s_sign, b_s)
        each(s_above, b_s)
        each(v_sum, a_v[:EARLY_V])
        equal(1)
        v_flags(b_v[0])
        behind(1)
        v_flags(b_v[1])
        start(1)
        each(v_flags, b_v[2:])
        dma("Y", T.qw[:].bitcast(dt.uint8), T.wc[:], [R("xv", 6, 7)], [R("qw", 0, 512)], 8.0)
        dma("Y", T.sw[:], T.ws[:], [], [R("sw", 0, 512)], 8.0)
        dma("Y", T.vt[:], T.v[:], [], [R("vt", 0, 512)], 20.0)
        each(v_sum, b_v)
        each(v_flags, a_v[EARLY_V:EARLY_V + MID_V])
        scan(R("cs", 8, 8 + 8 * H), R("xv", 0, 8 * H), R("xs", 0, 8 * H), 0.0, OP.add, OP.subtract)
        each(s_above, a_s)
        each(s_below, a_s[:MID_S])
        act(R("cg", 0, C), (R("cs", 0, 8 + 8 * H), xc))
        each(s_below, a_s[MID_S:])
        each(s_rest, b_s)
        each(s_below, b_s)
        ends = R("sc", 8 * H - 1, 14 * H, H)
        cp(sub(o_bv, 0, 7), ends)
        tt(base, init, R("iot", 78, 106), OP.add)
        each(v_flags, a_v[EARLY_V + MID_V:])
        turn(R("ct", 0, C), R("cg", 0, C))
        each(v_sum, a_v[EARLY_V:])
        tt(sub(dif, 0, nsa), sub(base, 0, nsa), sub(gt, 0, nsa), OP.subtract)
        scan(R("cu", 0, C), R("c32", 0, C), R("ct", 0, C), 0.0, OP.mult, OP.add)
        cp(sub(pre, nsa, hk), R("sc", hh * nsa + hh - 1, hh * hk, hh))
        tt(sub(pre, 0, nsa), sub(dif, 0, nsa), sub(lt, 0, nsa), OP.add)
        tt(sub(dif, hk, hk + 7), sub(base, hk, hk + 7), sub(gt, hk, hk + 7), OP.subtract)
        tt(sub(out, 0, hk), sub(pre, 0, hk), R("cu", 31, C, 32), OP.subtract)
        cp((R("g0", 0, C), sub(o_bv, 0, 7)), R("jrow", 16 * b_v[0], C))
        cp(o_a, sub(out, 0, hk))
        tt(sub(out, hk, hk + 7), sub(dif, hk, hk + 7), sub(lt, hk, hk + 7), OP.add)
        cp(sub(o_bs, 0, 7), sub(out, hk, hk + 7))
        cp((R("g0", 0, C), o_a), R("jrow", 0, H))
        cp((R("g0", 0, C), sub(o_bs, 0, 7)), R("jrow", H, 16 * b_v[0]))
        cp(sub(out, b_v[0], 28), ends)
        return out

    def diag(out, a):
        scan(out, R("cdg", 0, H), a, 1.0, OP.mult, OP.min)

    def to_offsets(row, j):
        o = of(28)
        for i in range(2):
            diag(R("dgb", C * j + H * i, C * j + H * i + H), sub(row, H * i, H * i + H))
        ts(o, R("dgb", C * j + 15, C * j + C, 16), col(3), OP.mult, -1.0, OP.add)
        return o

    def halved(a, w):
        i0, i1 = R("si", sip[0], sip[0] + w), R("si", sip[0] + w, sip[0] + 2 * w)
        sip[0] += 2 * w
        o = of(w)
        cp(i0, a)
        ts(i1, i0, 1, OP.arith_shift_right)
        ts(o, i1, 224.0, OP.min)
        return o

    r0 = first_ranks()
    act(R("cbig", 0, 464), R("mask", 0, 464), AF.Copy, None, BIG)
    tb = (0, 1, 6, 7)
    for t in range(4):
        mm(bank(tb[t], C), R("qe", 128 * t, 128 * t + 128), R("se", 128 * t, 128 * t + 128), R("qx", 0, C), R("sx", 0, C))
    act(R("idr", 0, H), R("jrow", 0, H), AF.Copy, None, 2.0 ** -17)
    diag(R("dg", 0, H), R("g0", 0, C, 2))
    diag(R("dg", H, C), R("g0", 1, C, 2))
    l0 = of(28)
    ts(l0, R("dg", 15, C, 16), col(3), OP.mult, -1.0, OP.add)
    aside(True)
    for t in range(4):
        mov("SSVV"[t], plane("t8", C, t), bank(tb[t], C), 0.125)
    aside(False)
    send("l0", {"l": ("of", l0[1])})
    cp(R("coff", 0, 42), R("iot", 8, 50))
    ts(xd, R("iot", 8, 36), col(0), OP.add, -15.0, OP.add)
    ts(xs1, R("iot", 50, 78), col(4), OP.add)
    ts(xs2, R("iot", 50, 78, 2), col(4), OP.add)
    gfill(R("g1", 0, 672), 1)
    gfill(R("at1", 0, HW), 225)
    cp(R("srow", 0, C, 2), (R("row0", 0, C), sub(l0, 0, 14)))
    cp(R("srow", 1, C, 2), (R("row0", 0, C), sub(l0, 14, 28)))
    o_r = of(28)
    ts(o_r, r0, 225.0, OP.add)
    scan(R("shold", 1, 465), R("cbig", 0, 464), R("srow", 0, 464), 0.0, OP.add, OP.min)
    act(R("sig1", 0, C), (R("srow", 0, 512), xs1))
    four("e", R("lq", 0, C), R("ls", 0, C), C)
    for t in range(4):
        mov("SVSV"[t], plane("tph", C, t), bank(2 + t, C), 0.5)


    def make_p(lst, win, ww, wn, first, zt, qi, pt, qp, sp):
        def ev(t, lo, hi):
            return plane("hp", HW, t, 225 + 2 * lo, 225 + 2 * hi, 2) if first else plane("ztmp", H, t, lo, hi)

        def pick(t, half, lo, hi):
            return (plane(win, ww, t, 0, wn), sub(lst, 14 * half + lo // 16, 14 * half + hi // 16))

        cp(ev(3, 0, H), pick(3, 0, 0, H))
        for j, (lo, hi, m0) in enumerate(RUNS):
            for t in range(3):
                act(ev(t, lo, hi), pick(t, 0, lo, hi))
            for t in range(4):
                tt(word(zt, t, lo, hi), pick(t, 1, lo, hi), ev(t, lo, hi), OP.add)
            quant(R("qa", H * qi + m0, H * qi + hi), R("sa", H * qi + m0, H * qi + hi), R(zt, 4 * m0, 4 * hi))
            four("w", R("qa", H * qi + m0, H * qi + hi), R("sa", H * qi + m0, H * qi + hi), hi - m0)
            for t in range(4):
                mov(COPIES[j][t], word(pt, t, lo, hi), bank(2 + t, hi - m0, lo - m0), 0.03125)
            quant(R(qp, m0, hi), R(sp, m0, hi), R(pt, 4 * m0, 4 * hi))
            for b in SCORES[j]:
                mm(bank(b, hi - m0), qr, sr, R(qp, m0, hi), R(sp, m0, hi))

    def merge(row, hold, w, xo, sig, creset, grow, gw, places):
        m1 = 14 * w
        hh, ns = H // 2, 14 - NVM[places == H]
        ob, off, o_v = of(28), of(14), of(14)
        cb, c2, c3, lt, gt, dif, own, a = (sm(14) for _ in range(8))
        ends = R("f1s", w - 1, m1, w)

        def held(k):
            return R(hold, 16 * k + 15, 16 * k + 16)

        def flags(k):
            e = 16 * k + 16
            ts(R("fl", H * k, H * k + e), R(row, 0, e), held(k), OP.is_le)
            if e < H:
                ts(R("fl", H * k + e, H * k + H), R(row, e, H), held(k), OP.is_lt)

        def total(k):
            scan(R("sc", hh * k, hh * k + hh), R("fl", H * k, H * k + hh), R("fl", H * k + hh, H * k + H), sub(c3, k, k + 1), OP.add, OP.add)

        for j, (lo, hi, m0) in enumerate(RUNS):
            b_v, b_s = (bank(b, hi - m0, lo - m0) for b in SCORES[j])
            act(R(row, lo, hi), b_s)
            tt(R("mm", lo, hi), b_v, R("mask", lo, hi), OP.mult)
            scan(R(hold, lo, hi), R("nmask", lo, hi), R("mm", lo, hi), 0.0, OP.mult, OP.add)
            act(R("pdup", 2 * lo, 2 * hi), (R(row, 0, hi), sub(xd, lo // 8, hi // 8)))
        for j, (lo, hi, m0) in enumerate(RUNS):
            k0, k1 = lo // 16, hi // 16
            end = R("f1s", w * k0 + w - 1, w * k1, w)
            tt(R("f1", w * k0, w * k1), (R(hold, 0, hi), sub(xo, w * k0 // 16, w * k1 // 16)), R(sig, w * k0, w * k1), OP.is_ge)
            tt(R("eq", lo, hi), bank(SCORES[j][0], hi - m0, lo - m0), R(hold, lo, hi), OP.is_equal)
            scan(R("f1s", w * k0, w * k1), R(creset, w * k0, w * k1), R("f1", w * k0, w * k1), 0.0, OP.mult, OP.add)
            ts(sub(ob, 2 * k0, 2 * k1, 2), end, 16.0, OP.mult, col(5), OP.max)
            ts(sub(ob, 2 * k0 + 1, 2 * k1, 2), end, 16.0, OP.mult, col(6), OP.max)
            tt(R("f2", 2 * lo, 2 * hi), (R("shold", 16, 465), sub(ob, 2 * k0, 2 * k1)), R("pdup", 2 * lo, 2 * hi), OP.is_le)
        scan(R("eup", 0, H), R("eq", 0, H), R("nmask", 0, H), 0.0, OP.add, OP.mult)
        for k in range(ns):
            act(R("sg", H * k, H * k + H), R(row, 0, H), AF.Sign, held(k), -1.0)
        for k in range(ns):
            lo = R("sg", H * k, H * k + 16 * k + 16)
            act(lo, lo, AF.Relu, None, -1.0, sub(gt, k, k + 1))
        for k in range(ns):
            hi = R("sg", H * k + 16 * k + 16, H * k + H)
            act(hi, hi, AF.Relu, None, None, sub(lt, k, k + 1))
        vs = list(range(ns, 14))
        turn(R("f2t", 0, C), R("f2", 0, C))
        ts(cb, ends, 16.0, OP.mult, -1.0, OP.add)
        flags(vs[0])
        scan(R("f2s", 0, C), R("c32", 0, C), R("f2t", 0, C), 0.0, OP.mult, OP.add)
        tt(c2, cb, R("eup", 15, H, 16), OP.subtract)
        flags(vs[1])
        tt(c3, c2, R("f2s", 31, C, 32), OP.add)
        for k in vs[2:]:
            flags(k)
        tt(sub(dif, 0, ns), R("iot", 78, 78 + ns), sub(gt, 0, ns), OP.subtract)
        for k in vs:
            total(k)
        tt(sub(own, 0, ns), sub(dif, 0, ns), sub(c3, 0, ns), OP.add)
        sums = R("sc", hh * ns + hh - 1, hh * 14, hh)
        cp(sub(o_v, 0, 14 - ns), sums)
        tt(sub(a, 0, ns), sub(own, 0, ns), sub(lt, 0, ns), OP.add)
        cp((R(grow, 0, gw), sub(o_v, 0, 14 - ns)), R("idr", 16 * ns, H))
        cp(sub(off, 0, ns), sub(a, 0, ns))
        cp(sub(a, ns, 14), sums)
        cp((R(grow, 0, gw), sub(off, 0, ns)), R("idr", 0, 16 * ns))
        nk, st = places // 16, places // H
        d1, d2, lst = sm(nk), sm(nk), of(nk)
        scan(R("cum", 0, places), R(grow, 0, places), R(grow, 0, places), 224.0, OP.add, OP.max)
        for j in range(st):
            diag(R("dgb", H * j, H * j + H), R(grow, j, places, st))
        for j in range(st):
            diag(R("dgc", H * j, H * j + H), R("cum", j, places, st))
            if j == 0:
                ts(d1, R("dgb", 15, places, 16), 2.0 ** 17, OP.mult)
        tt(d2, d1, R("dgc", 15, places, 16), OP.min)
        ts(lst, d2, col(3), OP.mult)
        return a, lst

    make_p(R("ll", 0, 28), "tph", C, C, True, "z1", 0, "p1", "qp1", "sp1")
    send("mp", {"q": ("qp1", 0), "s": ("sp1", 0)})
    gfill(R("g2", 0, 496), 1)
    gfill(R("at2", 0, HW), 225)
    a1, l1 = merge("row1", "hold1", 32, x1, "sig1", "c32", "g1", 672, C)
    send("l1", {"l": ("of", l1[1])})
    for t in range(4):
        act(plane("hp", HW, t, 226, 674, 2), (plane("tph", C, t), R("ll", 14, 28)))
    four("e", R("lq", C, C + H), R("ls", C, C + H), H)
    for t in range(4):
        act(plane("hp", HW, t, 1, 225), bank(2 + t, H), AF.Copy, None, 0.5)
    cp((R("at1", 0, HW), sub(l1, 0, 14)), R("jrow", 0, H))
    cp((R("at1", 0, HW), sub(l1, 14, 28)), R("jrow", 0, H))
    o_b1 = halved(a1, 14)
    send("k1", {"l": ("of", o_b1[1])})
    act(R("sig2", 0, H), (R("srow", 0, 512), xs2))
    act(R("c16", 0, H), R("tm", 0, H), AF.Sign)
    for t in range(4):
        for j in range(2):
            mov("SSSV"[t], plane("ho", OW, t, 225 + j, 449, 2), (plane("t8", C, t), sub(l0, 14 * j, 14 * j + 7)), 8.0)
    act(R("ag1", 0, C), (R("at1", 0, HW), o_r))
    o_x0 = halved(r0, 28)
    o_x1 = to_offsets(R("ag1", 0, C), 1)
    quant(R("qv", 0, 128), R("sv", 0, 128), R("vt", 0, 512))

    make_p(R("ll", 32, 60), "hp", HW, 673, False, "z2", 1, "p2", "qp2", "sp2")
    a2, l2 = merge("row2", "hold2", 16, x2, "sig2", "c16", "g2", 496, H)
    four("e", R("qp2", 0, H), R("sp2", 0, H), H)
    for t in range(4):
        act(plane("ho", OW, t, 1, 225), bank(2 + t, H))
    o_b2 = of(14)
    ts(o_b2, a2, 224.0, OP.min)
    send("k2", {"l": ("of", o_b2[1])})
    for nm in ("b2", "b1"):
        fill(R(nm, 4 * H, 4 * BW), 0.0)

    def products(w, j, q_, s_):
        for b in range(4):
            mm(bank(BANKS[j][b], size(q_)), R("q" + w, 128 * b, 128 * b + 128), R("s" + w, 128 * b, 128 * b + 128), q_, s_)

    for j, (lo, hi, m0) in enumerate(BACK):
        for t in range(4):
            mov("SV"[t % 2], word("e2", t, lo, hi), (plane("ho", OW, t, 0, 449), sub(l2, lo // 16, hi // 16)))
        q0 = (2 + j) * H
        quant(R("qa", q0, q0 + hi - m0), R("sa", q0, q0 + hi - m0), R("e2", 4 * m0, 4 * hi))
        products("w", j, R("qa", q0, q0 + hi - m0), R("sa", q0, q0 + hi - m0))

    def hand_back(k, bt, qb, sb, msg, vals, kv):
        for j, (lo, hi, m0) in enumerate(BACK):
            for t in range(4):
                mov("SV"[t % 2], word(bt, t, lo, hi), bank(BANKS[j][t], hi - m0, lo - m0), k)
            end = max(hi, lo + 128)
            quant(R(qb, lo, end), R(sb, lo, end), R(bt, 4 * lo, 4 * end))
        aside(True)
        send(msg, {"q": (qb, 0), "s": (sb, 0)})
        for j, (lo, hi, m0) in enumerate(BACK):
            for t in range(4):
                act(plane(vals, VW, t, lo, hi), bank(BANKS[j][t], hi - m0, lo - m0), AF.Copy, None, kv)

    def landed(m):
        return R("ll", BASE[m], BASE[m] + 14)

    hand_back(0.03125, "b2", "qb2", "sb2", "m2", "v8", 2.0 ** -8)
    rid, pid = topo.addr(prv2, core)
    add("G", lambda q: q.remote_dma(T.ll[:, BASE["k3"]:BASE["k3"] + 14], ap(o_b2), T.sem.a_k3, T.sem.lsent, pid, rid, topo.mask(core, prv2)),
        [o_b2], [], ISSUE, remote="k3")
    sent[0] += len(topo.engines(core, prv2))
    cp((R("at2", 0, HW), l2), R("jrow", 0, H))
    aside(False)
    for nm in ("v8", "d1", "d0"):
        fill(R(nm, H, 4 * VW, VW), 0.0)
    fill(R("mr", H, 3 * VW, VW), 225.0)
    act(R("ag2", 0, C), (R("at2", 0, HW), o_r))
    o_x2 = to_offsets(R("ag2", 0, C), 2)
    jw = R("jrow", 0, 225)
    act(plane("mr", VW, 0, 0, H), (jw, landed("k2")))
    act(R("ix", 0, C), (plane("mr", VW, 0, 0, 225), o_x1))
    act(R("un", 0, C), R("ag2", 0, C), AF.Relu, -224.0, 1.0)
    for t in range(4):
        tt(plane("y2", C, t), (plane("v8", VW, t, 0, 225), o_x2), plane("t8", C, t), OP.add)

    for j, (lo, hi, m0) in enumerate(BACK):
        products("e", j, R("lq", C + H + m0, C + H + hi), R("ls", C + H + m0, C + H + hi))
    hand_back(None, "b1", "qb1", "sb1", "m1", "d1", 0.25)
    aside(False)
    o_y1 = to_offsets(R("ix", 0, C), 3)
    act(plane("mr", VW, 1, 0, H), (jw, landed("k3")))
    act(plane("mr", VW, 2, 0, H), (plane("mr", VW, 1, 0, 225), landed("k1")))
    act(R("ix", C, 2 * C), (plane("mr", VW, 2, 0, 225), o_x0))
    ts(R("un", C, 2 * C), R("ix", 0, C), 224.0, OP.max, -232.0, OP.add)
    scan(R("un", 3 * C, 4 * C), R("un", 0, C), R("un", C, 2 * C), -64.0, OP.max, OP.add)
    for t in range(4):
        tt(plane("y1", C, t), (plane("d1", VW, t, 0, 225), o_y1), plane("y2", C, t), OP.add)
    o_y0 = to_offsets(R("ix", C, 2 * C), 4)
    ts(R("un", 2 * C, 3 * C), R("ix", C, 2 * C), 224.0, OP.max, -232.0, OP.add)
    scan(R("un", 4 * C, 5 * C), R("un", 3 * C, 4 * C), R("un", 2 * C, 3 * C), -64.0, OP.max, OP.add)

    act(R("ucr", 0, C), R("un", 4 * C, 5 * C), AF.Identity, -13.0, -1.0)
    dma("Y", T.uc[:], T.ucr[0:128:16, :], [R("ucr", 0, C)], [], 6.0)

    four("e", R("lq", C + 2 * H, C + 3 * H), R("ls", C + 2 * H, C + 3 * H), H)
    for t in range(4):
        act(plane("d0", VW, t, 0, H), bank(2 + t, H), AF.Copy, None, 0.5)

    def last(j, ts_):
        lo, hi = CHUNKS[j]
        for t in ts_:
            tt(word("xf", t, lo, hi), (plane("d0", VW, t, 0, 225), sub(o_y0, lo // 16, hi // 16)), plane("y1", C, t, lo, hi), OP.add)

    last(0, (0,))
    for j, (lo, hi) in enumerate(CHUNKS):
        last(j, (1, 2, 3))
        if j + 1 < len(CHUNKS):
            last(j + 1, (0,))
        quant(R("qo", lo, hi), R("so", lo, hi), R("xf", 4 * lo, 4 * hi))
        mm(bank((0, 1, 6)[j], hi - lo), R("qv", 0, 128), R("sv", 0, 128), R("qo", lo, hi), R("so", lo, hi))
        dma("Y", T.oc[:, 4 * lo:4 * hi], T.qo[:, lo:hi].bitcast(dt.uint8), [R("qo", lo, hi)], [], 1.5 + OUT * (C - lo))
        act(R("yo", lo, hi), bank((0, 1, 6)[j], hi - lo))
        dma("S", T.y[:, lo:hi], T.yo[:, lo:hi], [R("yo", lo, hi)], [], 1.5 + OUT * (C - lo))
    for k in range(4):
        dma("Y", T.osc[4 * k:4 * k + 4, :], T.so[32 * k:32 * k + 4, :], [R("so", 0, C)], [], 1.6)
    emit()
